import numpy as np
import ml_dtypes


def mxq(x, axis, fmt="e4m3"):
    dtype, down = {"e4m3": (ml_dtypes.float8_e4m3fn, 7), "e5m2": (ml_dtypes.float8_e5m2, 14)}[fmt]
    v = np.moveaxis(np.asarray(x, np.float32).astype(ml_dtypes.bfloat16).astype(np.float64), axis, -1)
    blocks = v.reshape(v.shape[:-1] + (-1, 32))
    amax = np.abs(blocks).max(-1, keepdims=True)
    byte = np.maximum(np.where(amax > 0, np.frexp(amax)[1] - 1 + 127, 0) - down, 1)
    scale = np.exp2(byte - 127.0)
    codes = (blocks / scale).astype(np.float32).astype(dtype).astype(np.float64)
    return np.moveaxis((codes * scale).reshape(v.shape), -1, axis)


WIDE = False


def mx_kscale(k):
    if not WIDE:
        return np.ones(k)
    levels = np.array([10, -10, 5, -5, 0])
    if k % 512:
        return np.exp2(np.random.permutation(np.resize(levels, k // 32))).repeat(32)
    a = np.empty((k // 512, 16))
    for p in range(k // 512):
        a[p, :8] = np.random.permutation(np.resize(levels, 8))
        for g in range(8):
            far = levels[np.abs(levels - a[p, g]) >= 10]
            a[p, g + 8] = far[np.random.randint(len(far))]
    return np.exp2(a.ravel()).repeat(32)


def f64(x):
    return np.asarray(x).astype(np.float64)


def striped(idx):
    return np.tile(idx.reshape(-1, 16).T, (8, 1)).astype(np.uint16)


def unstriped(offs):
    return offs[:16].T.reshape(-1).astype(np.int64)


def pack_weight(w):
    k, n = w.shape
    w = f64(np.asarray(w, np.float32).astype(ml_dtypes.bfloat16)).reshape(k // 32, 32, n)
    amax = np.abs(w).max(1)
    byte = np.clip(np.where(amax > 0, np.frexp(amax)[1] - 1 + 127 - 7, 1), 1, 254)
    scaled = (w * np.exp2(127.0 - byte)[:, None, :]).reshape(k, n).astype(np.float32)
    words = np.ascontiguousarray(scaled.reshape(k // 512, 128, 4, n).transpose(0, 1, 3, 2)).astype(ml_dtypes.float8_e4m3fn).view(np.uint8)
    return words, np.ascontiguousarray(byte.astype(np.uint8).reshape(k // 512, 16, n))


def unpack_weight(words, scales):
    g, p, n, _ = words.shape
    vals = np.ascontiguousarray(words).view(ml_dtypes.float8_e4m3fn).astype(np.float64) * np.repeat(np.exp2(scales.astype(np.float64) - 127.0), 8, axis=1)[..., None]
    return vals.transpose(0, 1, 3, 2).reshape(g * 512, n)


def relu(v):
    return np.maximum(v, 0.0)


K, T, S, H, N = 512, 4096, 1024, 512, 256


def setup_inputs():
    n = np.random.standard_normal
    s = mx_kscale(K)[:, None]
    u = mx_kscale(H)
    packed_xT = pack_weight(n((K, T)) * s)
    packed_w1 = pack_weight(n((K, N)) / np.sqrt(2 * K) / s)
    packed_w3 = pack_weight(n((H, N)) / np.sqrt(2 * H) / u[:, None])
    return {
        "x_words": packed_xT[0],
        "x_scales": packed_xT[1],
        "w1_words": packed_w1[0],
        "w1_scales": packed_w1[1],
        "w2": (n((K, H)) / np.sqrt(K) / s * u).astype(np.float32),
        "w3_words": packed_w3[0],
        "w3_scales": packed_w3[1],
        "offs": striped(np.random.permutation(T)[:S]),
    }


def reference(x_words, x_scales, w1_words, w1_scales, w2, w3_words, w3_scales, offs):
    xq = unpack_weight(x_words, x_scales)[:, unstriped(offs)]
    h = relu(mxq(f64(w2), 0, "e4m3").T @ xq)
    return unpack_weight(w1_words, w1_scales).T @ xq + unpack_weight(w3_words, w3_scales).T @ mxq(h, 0, "e4m3")

@@ -1,0 +1,181 @@
+from contextlib import ExitStack
+
+import concourse.mybir as mybir
+
+K, T, S, H, N = 512, 4096, 1024, 512, 256
+FLOPS = 2 * S * (K * H + K * N + H * N)
+
+F32 = mybir.dt.float32
+BF16 = mybir.dt.bfloat16
+I32 = mybir.dt.int32
+U32 = mybir.dt.uint32
+U16 = mybir.dt.uint16
+U8 = mybir.dt.uint8
+FP8X4 = mybir.dt.float8_e4m3fn_x4
+RELU = mybir.ActivationFunctionType.Relu
+
+P = 128
+AL = 64
+H_ON_SCALAR = (0, 2, 3, 5, 6)
+O_ON_SCALAR = (0, 2)
+
+
+def tile_picked_lora_relu_p_kernel(
+    tc, x_words, x_scales, w1_words, w1_scales, w2, w3_words, w3_scales, offs, out
+):
+    nc = tc.nc
+    with ExitStack() as ctx:
+        keep = ctx.enter_context(tc.tile_pool(name="keep", bufs=1))
+        hps = ctx.enter_context(tc.psum_pool(name="hps", bufs=4))
+        ops = ctx.enter_context(tc.psum_pool(name="ops", bufs=1))
+
+        offsets = keep.tile([P, S // 16], U16, name="offsets")
+        nc.sync.dma_start(offsets[:], offs)
+
+        xs_win = keep.tile([P, T], U8, name="xs_win", tag="first", align_bytes=AL)
+        nc.vector.memset(xs_win[:].bitcast(I32), 0)
+        nc.scalar.dma_start(xs_win[0:P:8, :].bitcast(I32), x_scales[0].bitcast(I32))
+
+        w1c = keep.tile([P, N], U32, name="w1c", align_bytes=AL)
+        nc.sync.dma_start(w1c[:].bitcast(I32), w1_words[0].rearrange("p n t -> p (n t)").bitcast(I32))
+        xw_win = keep.tile([P, T], U32, name="xw_win", align_bytes=AL)
+        nc.sync.dma_start(xw_win[:].bitcast(I32), x_words[0].rearrange("p n t -> p (n t)").bitcast(I32))
+        w2v = w2.rearrange("(p j) c -> p j c", j=4)
+        raw = []
+        for hf in range(2):
+            r = keep.tile([P, 4, 256], F32, name="raw%d" % hf)
+            nc.sync.dma_start(r[:], w2v[:, :, 256 * hf : 256 * (hf + 1)])
+            raw.append(r)
+
+        w1s = keep.tile([P, N], U8, name="w1s", align_bytes=AL)
+        w3s = keep.tile([P, N], U8, name="w3s", align_bytes=AL)
+        xs = keep.tile([P, S], U8, name="xs", align_bytes=AL)
+        warm = keep.tile([P, 8], F32, name="warm")
+        warm2 = keep.tile([P, 8], F32, name="warm2")
+        nc.gpsimd.memset(w1s[:].bitcast(I32), 0)
+        for q in range(4):
+            nc.gpsimd.dma_start(w1s[32 * q : 32 * q + 4, :].bitcast(I32), w1_scales[0, 4 * q : 4 * q + 4, :].bitcast(I32))
+        nc.vector.memset(w3s[:].bitcast(I32), 0)
+        nc.vector.memset(xs[:].bitcast(I32), 0)
+        nc.vector.memset(warm[:], 0.0)
+        nc.scalar.activation(warm2[:], warm[:], RELU)
+        for q in range(4):
+            nc.gpsimd.dma_start(w3s[32 * q : 32 * q + 4, :].bitcast(I32), w3_scales[0, 4 * q : 4 * q + 4, :].bitcast(I32))
+
+        xs_g = keep.tile([P, S], U8, name="xs_g", tag="late", align_bytes=AL)
+        nc.vector.tensor_copy(xs_g[:], xs_win[:].indirect(offsets[:]))
+        for i in range(4):
+            nc.scalar.dma_start(xs[i:P:32, :].bitcast(I32), xs_g[8 * i : P : 32, :].bitcast(I32))
+        w3c = keep.tile([P, N], U32, name="w3c", tag="late", align_bytes=AL)
+        nc.sync.dma_start(w3c[:].bitcast(I32), w3_words[0].rearrange("p n t -> p (n t)").bitcast(I32))
+
+        obank = [ops.tile([P, 2, 256], F32, name="obank%d" % g) for g in range(4)]
+        xg = []
+        for hf in range(2):
+            g = keep.tile([P, 512], U32, name="xg%d" % hf, tag="first" if hf == 0 else "xg1", align_bytes=AL)
+            nc.vector.tensor_copy(g[:], xw_win[:].indirect(offsets[:, 32 * hf : 32 * (hf + 1)]))
+            xg.append(g)
+            for gi in range(2):
+                for mt in range(2):
+                    nc.tensor.matmul_mx(
+                        out=obank[2 * hf + gi][:, mt, :],
+                        lhsT=w1c[:, P * mt : P * (mt + 1)].bitcast(FP8X4),
+                        lhsT_scale=w1s[:, P * mt : P * (mt + 1)],
+                        rhs=g[:, 256 * gi : 256 * (gi + 1)].bitcast(FP8X4),
+                        rhs_scale=xs[:, 512 * hf + 256 * gi : 512 * hf + 256 * (gi + 1)],
+                        start=(mt == 0),
+                        stop=False,
+                    )
+
+        w2c = [keep.tile([P, P], U32, name="w2c%d" % t, align_bytes=AL) for t in range(4)]
+        w2s = [keep.tile([P, P], U8, name="w2s%d" % t, align_bytes=AL) for t in range(4)]
+        grp = {}
+
+        def cast(hf, tp, on_scalar):
+            gt = keep.tile([P, 2, 64, 4], BF16, name="grp%d%d" % (hf, tp), align_bytes=AL)
+            src = raw[hf][:].rearrange("p j (m t) -> p m t j", t=4)[:, :, 2 * tp : 2 * tp + 2, :]
+            dst = gt[:].rearrange("p t m j -> p m t j")
+            if on_scalar:
+                nc.scalar.copy(dst, src)
+            else:
+                nc.vector.tensor_copy(dst, src)
+            grp[(hf, tp)] = gt
+
+        def quant_w2(hf, tp):
+            for tt in range(2):
+                t = 2 * tp + tt
+                nc.vector.quantize_mx(
+                    out=w2c[t][:, 64 * hf : 64 * (hf + 1)].bitcast(FP8X4),
+                    scales=w2s[t][:, 64 * hf : 64 * (hf + 1)],
+                    in_=grp[(hf, tp)][:, tt, :, :].rearrange("p m j -> p (m j)"),
+                )
+
+        cast(0, 0, True)
+        cast(0, 1, True)
+        cast(1, 1, True)
+        quant_w2(0, 0)
+        cast(1, 0, False)
+        quant_w2(0, 1)
+        quant_w2(1, 0)
+        quant_w2(1, 1)
+
+        hq = [keep.tile([P, 256], U32, name="hq%d" % g, align_bytes=AL) for g in range(4)]
+        hs = [keep.tile([P, 256], U8, name="hs%d" % g, align_bytes=AL) for g in range(4)]
+        hb = {}
+        outv = out.rearrange("(a p) s -> p a s", a=2)
+
+        def first(c):
+            bank = hps.tile([P, 4, P], F32, name="hbank")
+            cols = slice(P * (c % 4), P * (c % 4 + 1))
+            for t in range(4):
+                nc.tensor.matmul_mx(
+                    out=bank[:, t, :],
+                    lhsT=w2c[t][:].bitcast(FP8X4),
+                    lhsT_scale=w2s[t][:],
+                    rhs=xg[c // 4][:, cols].bitcast(FP8X4),
+                    rhs_scale=xs[:, P * c : P * (c + 1)],
+                    start=True,
+                    stop=True,
+                )
+            b = keep.tile([P, P, 4], BF16, name="hb%d" % c, align_bytes=AL)
+            src = bank[:].rearrange("p t n -> p n t")
+            if c in H_ON_SCALAR:
+                nc.scalar.activation(b[:], src, RELU)
+            else:
+                nc.vector.tensor_scalar_max(b[:], src, 0.0)
+            hb[c] = b
+
+        def quant_h(c):
+            cols = slice(P * (c % 2), P * (c % 2 + 1))
+            nc.vector.quantize_mx(
+                out=hq[c // 2][:, cols].bitcast(FP8X4),
+                scales=hs[c // 2][:, cols],
+                in_=hb[c][:].rearrange("p n t -> p (n t)"),
+            )
+
+        def second(g):
+            for mt in range(2):
+                nc.tensor.matmul_mx(
+                    out=obank[g][:, mt, :],
+                    lhsT=w3c[:, P * mt : P * (mt + 1)].bitcast(FP8X4),
+                    lhsT_scale=w3s[:, P * mt : P * (mt + 1)],
+                    rhs=hq[g][:].bitcast(FP8X4),
+                    rhs_scale=hs[g][:],
+                    start=False,
+                    stop=(mt == 1),
+                )
+            o = keep.tile([P, 2, 256], F32, name="o%d" % g)
+            if g in O_ON_SCALAR:
+                nc.scalar.copy(o[:], obank[g][:])
+            else:
+                nc.vector.tensor_copy(o[:], obank[g][:])
+            nc.sync.dma_start(outv[:, :, 256 * g : 256 * (g + 1)], o[:])
+
+        for c in range(8):
+            first(c)
+            if c >= 1:
+                quant_h(c - 1)
+            if c >= 3 and c % 2 == 1:
+                second((c - 3) // 2)
+        quant_h(7)
+        second(3)

@@ -15,9 +15,28 @@ FP8X4 = mybir.dt.float8_e4m3fn_x4
 RELU = mybir.ActivationFunctionType.Relu
 
 P = 128
-AL = 64
-H_ON_SCALAR = (0, 2, 3, 5, 6)
-O_ON_SCALAR = (0, 2)
+PACK = 4
+BLOCKS = K // 32
+ALIGN = 64
+HALF = S // 2
+CHUNK = 128
+CHUNKS = S // CHUNK
+PAIR = 2 * CHUNK
+W2_HALF = H // 2
+M_HALF = W2_HALF // PACK
+H_BANKS = 5
+OUT_BANKS = 8 - H_BANKS
+WARM_PASSES = 3
+GROUPS = [(0, 2), (2, 4), (4, 6), (6, 7), (7, 8)]
+
+
+def words_of(packed):
+    return packed[0].rearrange("p n t -> p (n t)").bitcast(I32)
+
+
+def place_scale_rows(nc, plane, rows):
+    for q in range(1, 4):
+        nc.sync.dma_start(plane[32 * q : 32 * q + PACK, :], rows[PACK * q : PACK * (q + 1), :])
 
 
 def tile_picked_lora_relu_p_kernel(
@@ -26,156 +45,158 @@ def tile_picked_lora_relu_p_kernel(
     nc = tc.nc
     with ExitStack() as ctx:
         keep = ctx.enter_context(tc.tile_pool(name="keep", bufs=1))
-        hps = ctx.enter_context(tc.psum_pool(name="hps", bufs=4))
-        ops = ctx.enter_context(tc.psum_pool(name="ops", bufs=1))
+        shared = ctx.enter_context(tc.tile_pool(name="shared", bufs=1))
+        h_psum = ctx.enter_context(tc.psum_pool(name="h_psum", bufs=H_BANKS))
+        out_psum = ctx.enter_context(tc.psum_pool(name="out_psum", bufs=OUT_BANKS))
 
+        xs_rows = keep.tile([BLOCKS, T], U8, name="xs_rows", align_bytes=ALIGN)
+        nc.sync.dma_start(xs_rows[:].bitcast(I32), x_scales[0].bitcast(I32))
+        ws_rows = keep.tile([BLOCKS, 2, N], U8, name="ws_rows", align_bytes=ALIGN)
+        for term, scales in enumerate((w1_scales, w3_scales)):
+            nc.scalar.dma_start(ws_rows[:, term, :].bitcast(I32), scales[0].bitcast(I32))
         offsets = keep.tile([P, S // 16], U16, name="offsets")
         nc.sync.dma_start(offsets[:], offs)
+        xw_table = keep.tile([P, T], U32, name="xw_table", align_bytes=ALIGN)
+        nc.sync.dma_start(xw_table[:].bitcast(I32), words_of(x_words))
+        w2_rows = w2.rearrange("(p j) c -> p j c", j=PACK)
+        w2_raw = []
+        for half in range(2):
+            raw = keep.tile([P, PACK, W2_HALF], F32, name="w2_raw%d" % half)
+            nc.sync.dma_start(raw[:], w2_rows[:, :, W2_HALF * half : W2_HALF * (half + 1)])
+            w2_raw.append(raw)
 
-        xs_win = keep.tile([P, T], U8, name="xs_win", tag="first", align_bytes=AL)
-        nc.vector.memset(xs_win[:].bitcast(I32), 0)
-        nc.scalar.dma_start(xs_win[0:P:8, :].bitcast(I32), x_scales[0].bitcast(I32))
+        xs_table = shared.tile([P, T], U8, name="xs_table", offset=0, align_bytes=ALIGN)
+        nc.vector.memset(xs_table[:].bitcast(I32), 0)
+        xs_plane = keep.tile([P, S], U8, name="xs_plane", align_bytes=ALIGN)
+        nc.vector.memset(xs_plane[:].bitcast(I32), 0)
+        ws_plane = keep.tile([P, 2, N], U8, name="ws_plane", align_bytes=ALIGN)
+        ws_plane_i32 = ws_plane[:].rearrange("p a n -> p (a n)").bitcast(I32)
+        ws_rows_i32 = ws_rows[:].rearrange("p a n -> p (a n)").bitcast(I32)
+        nc.vector.memset(ws_plane_i32, 0)
+        warm_in = keep.tile([P, 8], F32, name="warm_in")
+        warm_out = keep.tile([P, 8], F32, name="warm_out")
+        nc.vector.memset(warm_in[:], 0.0)
+        nc.scalar.activation(warm_out[:], warm_in[:], RELU)
+        nc.vector.tensor_copy(xs_table[0:BLOCKS, :].bitcast(I32), xs_rows[:].bitcast(I32))
+        nc.vector.tensor_copy(ws_plane_i32[0:PACK, :], ws_rows_i32[0:PACK, :])
+        place_scale_rows(nc, ws_plane_i32, ws_rows_i32)
 
-        w1c = keep.tile([P, N], U32, name="w1c", align_bytes=AL)
-        nc.sync.dma_start(w1c[:].bitcast(I32), w1_words[0].rearrange("p n t -> p (n t)").bitcast(I32))
-        xw_win = keep.tile([P, T], U32, name="xw_win", align_bytes=AL)
-        nc.sync.dma_start(xw_win[:].bitcast(I32), x_words[0].rearrange("p n t -> p (n t)").bitcast(I32))
-        w2v = w2.rearrange("(p j) c -> p j c", j=4)
-        raw = []
-        for hf in range(2):
-            r = keep.tile([P, 4, 256], F32, name="raw%d" % hf)
-            nc.sync.dma_start(r[:], w2v[:, :, 256 * hf : 256 * (hf + 1)])
-            raw.append(r)
+        xs_picked = keep.tile([P, S], U8, name="xs_picked", align_bytes=ALIGN)
+        nc.vector.tensor_copy(xs_picked[:], xs_table[:].indirect(offsets[:]))
+        place_scale_rows(nc, xs_plane[:].bitcast(I32), xs_picked[:].bitcast(I32))
+        nc.vector.tensor_copy(xs_plane[0:PACK, :].bitcast(I32), xs_picked[0:PACK, :].bitcast(I32))
+        w_words = []
+        for term, packed in enumerate((w1_words, w3_words)):
+            words = shared.tile([P, N], U32, name="w_words%d" % term, offset=4 * N * term, align_bytes=ALIGN)
+            nc.sync.dma_start(words[:].bitcast(I32), words_of(packed))
+            w_words.append(words)
 
-        w1s = keep.tile([P, N], U8, name="w1s", align_bytes=AL)
-        w3s = keep.tile([P, N], U8, name="w3s", align_bytes=AL)
-        xs = keep.tile([P, S], U8, name="xs", align_bytes=AL)
-        warm = keep.tile([P, 8], F32, name="warm")
-        warm2 = keep.tile([P, 8], F32, name="warm2")
-        nc.gpsimd.memset(w1s[:].bitcast(I32), 0)
-        for q in range(4):
-            nc.gpsimd.dma_start(w1s[32 * q : 32 * q + 4, :].bitcast(I32), w1_scales[0, 4 * q : 4 * q + 4, :].bitcast(I32))
-        nc.vector.memset(w3s[:].bitcast(I32), 0)
-        nc.vector.memset(xs[:].bitcast(I32), 0)
-        nc.vector.memset(warm[:], 0.0)
-        nc.scalar.activation(warm2[:], warm[:], RELU)
-        for q in range(4):
-            nc.gpsimd.dma_start(w3s[32 * q : 32 * q + 4, :].bitcast(I32), w3_scales[0, 4 * q : 4 * q + 4, :].bitcast(I32))
+        xw_picked = []
+        for half in range(2):
+            picked = keep.tile([P, HALF], U32, name="xw_picked%d" % half, align_bytes=ALIGN)
+            entries = offsets[:, HALF // 16 * half : HALF // 16 * (half + 1)]
+            nc.vector.tensor_copy(picked[:], xw_table[:].indirect(entries))
+            xw_picked.append(picked)
 
-        xs_g = keep.tile([P, S], U8, name="xs_g", tag="late", align_bytes=AL)
-        nc.vector.tensor_copy(xs_g[:], xs_win[:].indirect(offsets[:]))
-        for i in range(4):
-            nc.scalar.dma_start(xs[i:P:32, :].bitcast(I32), xs_g[8 * i : P : 32, :].bitcast(I32))
-        w3c = keep.tile([P, N], U32, name="w3c", tag="late", align_bytes=AL)
-        nc.sync.dma_start(w3c[:].bitcast(I32), w3_words[0].rearrange("p n t -> p (n t)").bitcast(I32))
-
-        obank = [ops.tile([P, 2, 256], F32, name="obank%d" % g) for g in range(4)]
-        xg = []
-        for hf in range(2):
-            g = keep.tile([P, 512], U32, name="xg%d" % hf, tag="first" if hf == 0 else "xg1", align_bytes=AL)
-            nc.vector.tensor_copy(g[:], xw_win[:].indirect(offsets[:, 32 * hf : 32 * (hf + 1)]))
-            xg.append(g)
-            for gi in range(2):
-                for mt in range(2):
-                    nc.tensor.matmul_mx(
-                        out=obank[2 * hf + gi][:, mt, :],
-                        lhsT=w1c[:, P * mt : P * (mt + 1)].bitcast(FP8X4),
-                        lhsT_scale=w1s[:, P * mt : P * (mt + 1)],
-                        rhs=g[:, 256 * gi : 256 * (gi + 1)].bitcast(FP8X4),
-                        rhs_scale=xs[:, 512 * hf + 256 * gi : 512 * hf + 256 * (gi + 1)],
-                        start=(mt == 0),
-                        stop=False,
-                    )
-
-        w2c = [keep.tile([P, P], U32, name="w2c%d" % t, align_bytes=AL) for t in range(4)]
-        w2s = [keep.tile([P, P], U8, name="w2s%d" % t, align_bytes=AL) for t in range(4)]
-        grp = {}
-
-        def cast(hf, tp, on_scalar):
-            gt = keep.tile([P, 2, 64, 4], BF16, name="grp%d%d" % (hf, tp), align_bytes=AL)
-            src = raw[hf][:].rearrange("p j (m t) -> p m t j", t=4)[:, :, 2 * tp : 2 * tp + 2, :]
-            dst = gt[:].rearrange("p t m j -> p m t j")
-            if on_scalar:
-                nc.scalar.copy(dst, src)
-            else:
-                nc.vector.tensor_copy(dst, src)
-            grp[(hf, tp)] = gt
-
-        def quant_w2(hf, tp):
-            for tt in range(2):
-                t = 2 * tp + tt
-                nc.vector.quantize_mx(
-                    out=w2c[t][:, 64 * hf : 64 * (hf + 1)].bitcast(FP8X4),
-                    scales=w2s[t][:, 64 * hf : 64 * (hf + 1)],
-                    in_=grp[(hf, tp)][:, tt, :, :].rearrange("p m j -> p (m j)"),
-                )
-
-        cast(0, 0, True)
-        cast(0, 1, True)
-        cast(1, 1, True)
-        quant_w2(0, 0)
-        cast(1, 0, False)
-        quant_w2(0, 1)
-        quant_w2(1, 0)
-        quant_w2(1, 1)
-
-        hq = [keep.tile([P, 256], U32, name="hq%d" % g, align_bytes=AL) for g in range(4)]
-        hs = [keep.tile([P, 256], U8, name="hs%d" % g, align_bytes=AL) for g in range(4)]
-        hb = {}
-        outv = out.rearrange("(a p) s -> p a s", a=2)
-
-        def first(c):
-            bank = hps.tile([P, 4, P], F32, name="hbank")
-            cols = slice(P * (c % 4), P * (c % 4 + 1))
-            for t in range(4):
-                nc.tensor.matmul_mx(
-                    out=bank[:, t, :],
-                    lhsT=w2c[t][:].bitcast(FP8X4),
-                    lhsT_scale=w2s[t][:],
-                    rhs=xg[c // 4][:, cols].bitcast(FP8X4),
-                    rhs_scale=xs[:, P * c : P * (c + 1)],
-                    start=True,
-                    stop=True,
-                )
-            b = keep.tile([P, P, 4], BF16, name="hb%d" % c, align_bytes=AL)
-            src = bank[:].rearrange("p t n -> p n t")
-            if c in H_ON_SCALAR:
-                nc.scalar.activation(b[:], src, RELU)
-            else:
-                nc.vector.tensor_scalar_max(b[:], src, 0.0)
-            hb[c] = b
-
-        def quant_h(c):
-            cols = slice(P * (c % 2), P * (c % 2 + 1))
-            nc.vector.quantize_mx(
-                out=hq[c // 2][:, cols].bitcast(FP8X4),
-                scales=hs[c // 2][:, cols],
-                in_=hb[c][:].rearrange("p n t -> p (n t)"),
+        warm_bank = out_psum.tile([P, HALF], F32, name="out_bank")
+        for warm_pass in range(WARM_PASSES):
+            nc.tensor.matmul_mx(
+                out=warm_bank[:],
+                lhsT=xw_picked[0][:, 0:P].bitcast(FP8X4),
+                lhsT_scale=xs_picked[:, 0:P],
+                rhs=xw_picked[0][:].bitcast(FP8X4),
+                rhs_scale=xs_picked[:, 0:HALF],
+                start=True,
+                stop=True,
             )
 
-        def second(g):
-            for mt in range(2):
-                nc.tensor.matmul_mx(
-                    out=obank[g][:, mt, :],
-                    lhsT=w3c[:, P * mt : P * (mt + 1)].bitcast(FP8X4),
-                    lhsT_scale=w3s[:, P * mt : P * (mt + 1)],
-                    rhs=hq[g][:].bitcast(FP8X4),
-                    rhs_scale=hs[g][:],
-                    start=False,
-                    stop=(mt == 1),
-                )
-            o = keep.tile([P, 2, 256], F32, name="o%d" % g)
-            if g in O_ON_SCALAR:
-                nc.scalar.copy(o[:], obank[g][:])
-            else:
-                nc.vector.tensor_copy(o[:], obank[g][:])
-            nc.sync.dma_start(outv[:, :, 256 * g : 256 * (g + 1)], o[:])
+        w2_words = [keep.tile([P, P], U32, name="w2_words%d" % t, align_bytes=ALIGN) for t in range(PACK)]
+        w2_plane = [keep.tile([P, P], U8, name="w2_plane%d" % t, align_bytes=ALIGN) for t in range(PACK)]
+        w2_bf16 = {}
 
-        for c in range(8):
-            first(c)
-            if c >= 1:
-                quant_h(c - 1)
-            if c >= 3 and c % 2 == 1:
-                second((c - 3) // 2)
-        quant_h(7)
-        second(3)
+        def round_w2(half, t0, copy):
+            rounded = keep.tile([P, 2, M_HALF, PACK], BF16, name="w2_bf16_%d_%d" % (half, t0), align_bytes=ALIGN)
+            source = w2_raw[half][:].rearrange("p j (m t) -> p m t j", t=PACK)[:, :, t0 : t0 + 2, :]
+            copy(rounded[:].rearrange("p t m j -> p m t j"), source)
+            w2_bf16[(half, t0)] = rounded
+
+        def quantise_w2(half, t0):
+            cols = slice(M_HALF * half, M_HALF * (half + 1))
+            for t in (t0, t0 + 1):
+                nc.vector.quantize_mx(
+                    out=w2_words[t][:, cols].bitcast(FP8X4),
+                    scales=w2_plane[t][:, cols],
+                    in_=w2_bf16[(half, t0)][:, t - t0, :, :].rearrange("p m j -> p (m j)"),
+                )
+
+        round_w2(0, 0, nc.scalar.copy)
+        round_w2(0, 2, nc.scalar.copy)
+        round_w2(1, 2, nc.scalar.copy)
+        quantise_w2(0, 0)
+        round_w2(1, 0, nc.vector.tensor_copy)
+        quantise_w2(0, 2)
+        quantise_w2(1, 0)
+        quantise_w2(1, 2)
+
+        def token_words(c0, c1):
+            first = CHUNK * c0 % HALF
+            return xw_picked[CHUNK * c0 // HALF][:, first : first + CHUNK * (c1 - c0)].bitcast(FP8X4)
+
+        h_words = [keep.tile([P, PAIR], U32, name="h_words%d" % g, align_bytes=ALIGN) for g in range(S // PAIR)]
+        h_plane = [keep.tile([P, PAIR], U8, name="h_plane%d" % g, align_bytes=ALIGN) for g in range(S // PAIR)]
+        for pair in range(S // PAIR):
+            h_bf16 = []
+            for c in (2 * pair, 2 * pair + 1):
+                h_bank = h_psum.tile([P, PACK, CHUNK], F32, name="h_bank")
+                for t in range(PACK):
+                    nc.tensor.matmul_mx(
+                        out=h_bank[:, t, :],
+                        lhsT=w2_words[t][:].bitcast(FP8X4),
+                        lhsT_scale=w2_plane[t][:],
+                        rhs=token_words(c, c + 1),
+                        rhs_scale=xs_plane[:, CHUNK * c : CHUNK * (c + 1)],
+                        start=True,
+                        stop=True,
+                    )
+                rounded = keep.tile([P, CHUNK, PACK], BF16, name="h_bf16_%d" % c, align_bytes=ALIGN)
+                sums = h_bank[:].rearrange("p t n -> p n t")
+                if c % 2 == 1 and c < CHUNKS - 1:
+                    nc.vector.tensor_scalar_max(rounded[:], sums, 0.0)
+                else:
+                    nc.scalar.activation(rounded[:], sums, RELU)
+                h_bf16.append(rounded)
+            for i in range(2):
+                cols = slice(CHUNK * i, CHUNK * (i + 1))
+                nc.vector.quantize_mx(
+                    out=h_words[pair][:, cols].bitcast(FP8X4),
+                    scales=h_plane[pair][:, cols],
+                    in_=h_bf16[i][:].rearrange("p n t -> p (n t)"),
+                )
+
+        out_tiles = out.rearrange("(a p) s -> p a s", p=P)
+        for g, (c0, c1) in enumerate(GROUPS):
+            width = CHUNK * (c1 - c0)
+            out_bank = out_psum.tile([P, HALF], F32, name="out_bank")
+            sums = out_bank[:, 0 : 2 * width].rearrange("p (a s) -> p a s", a=2)
+            h_cols = slice(CHUNK * (c0 % 2), CHUNK * (c0 % 2) + width)
+            moving = (
+                (token_words(c0, c1), xs_plane[:, CHUNK * c0 : CHUNK * c1]),
+                (h_words[c0 // 2][:, h_cols].bitcast(FP8X4), h_plane[c0 // 2][:, h_cols]),
+            )
+            for term, (words, plane) in enumerate(moving):
+                for a in range(2):
+                    nc.tensor.matmul_mx(
+                        out=sums[:, a, :],
+                        lhsT=w_words[term][:, P * a : P * (a + 1)].bitcast(FP8X4),
+                        lhsT_scale=ws_plane[:, term, P * a : P * (a + 1)],
+                        rhs=words,
+                        rhs_scale=plane,
+                        start=(term == 0 and a == 0),
+                        stop=(term == 1 and a == 1),
+                    )
+            result = keep.tile([P, 2, width], F32, name="result%d" % g)
+            if g >= 2 and g % 2 == 0:
+                nc.vector.tensor_copy(result[:], sums)
+            else:
+                nc.scalar.copy(result[:], sums)
+            nc.sync.dma_start(out_tiles[:, :, CHUNK * c0 : CHUNK * c1], result[:])

@@ -112,31 +112,26 @@ def tile_picked_lora_relu_p_kernel(
 
         w2_words = [keep.tile([P, P], U32, name="w2_words%d" % t, align_bytes=ALIGN) for t in range(PACK)]
         w2_plane = [keep.tile([P, P], U8, name="w2_plane%d" % t, align_bytes=ALIGN) for t in range(PACK)]
-        w2_bf16 = {}
+        w2_bf16 = [keep.tile([P, PACK, M_HALF, PACK], BF16, name="w2_bf16_%d" % half, align_bytes=ALIGN) for half in range(2)]
 
-        def round_w2(half, t0, copy):
-            rounded = keep.tile([P, 2, M_HALF, PACK], BF16, name="w2_bf16_%d_%d" % (half, t0), align_bytes=ALIGN)
-            source = w2_raw[half][:].rearrange("p j (m t) -> p m t j", t=PACK)[:, :, t0 : t0 + 2, :]
-            copy(rounded[:].rearrange("p t m j -> p m t j"), source)
-            w2_bf16[(half, t0)] = rounded
+        def round_w2(half, columns, copy):
+            source = w2_raw[half][:].rearrange("p j (m t) -> p m j t", t=PACK)
+            copy(w2_bf16[half][:].rearrange("p t m j -> p m j t")[:, columns, :, :], source[:, columns, :, :])
 
-        def quantise_w2(half, t0):
+        def quantise_w2(half):
             cols = slice(M_HALF * half, M_HALF * (half + 1))
-            for t in (t0, t0 + 1):
+            for t in range(PACK):
                 nc.vector.quantize_mx(
                     out=w2_words[t][:, cols].bitcast(FP8X4),
                     scales=w2_plane[t][:, cols],
-                    in_=w2_bf16[(half, t0)][:, t - t0, :, :].rearrange("p m j -> p (m j)"),
+                    in_=w2_bf16[half][:, t, :, :].rearrange("p m j -> p (m j)"),
                 )
 
-        round_w2(0, 0, nc.scalar.copy)
-        round_w2(0, 2, nc.scalar.copy)
-        round_w2(1, 2, nc.scalar.copy)
-        quantise_w2(0, 0)
-        round_w2(1, 0, nc.vector.tensor_copy)
-        quantise_w2(0, 2)
-        quantise_w2(1, 0)
-        quantise_w2(1, 2)
+        round_w2(0, slice(0, M_HALF), nc.scalar.copy)
+        round_w2(1, slice(0, M_HALF // 2), nc.scalar.copy)
+        round_w2(1, slice(M_HALF // 2, M_HALF), nc.vector.tensor_copy)
+        quantise_w2(0)
+        quantise_w2(1)
 
         def token_words(c0, c1):
             first = CHUNK * c0 % HALF

@@ -50,10 +50,7 @@ def tile_picked_lora_relu_p_kernel(
         out_psum = ctx.enter_context(tc.psum_pool(name="out_psum", bufs=OUT_BANKS))
 
         xs_rows = keep.tile([BLOCKS, T], U8, name="xs_rows", align_bytes=ALIGN)
-        nc.sync.dma_start(xs_rows[:].bitcast(I32), x_scales[0].bitcast(I32))
-        ws_rows = keep.tile([BLOCKS, 2, N], U8, name="ws_rows", align_bytes=ALIGN)
-        for term, scales in enumerate((w1_scales, w3_scales)):
-            nc.scalar.dma_start(ws_rows[:, term, :].bitcast(I32), scales[0].bitcast(I32))
+        nc.scalar.dma_start(xs_rows[:].bitcast(I32), x_scales[0].bitcast(I32))
         offsets = keep.tile([P, S // 16], U16, name="offsets")
         nc.sync.dma_start(offsets[:], offs)
         xw_table = keep.tile([P, T], U32, name="xw_table", align_bytes=ALIGN)
@@ -71,25 +68,28 @@ def tile_picked_lora_relu_p_kernel(
         nc.vector.memset(xs_plane[:].bitcast(I32), 0)
         ws_plane = keep.tile([P, 2, N], U8, name="ws_plane", align_bytes=ALIGN)
         ws_plane_i32 = ws_plane[:].rearrange("p a n -> p (a n)").bitcast(I32)
-        ws_rows_i32 = ws_rows[:].rearrange("p a n -> p (a n)").bitcast(I32)
         nc.vector.memset(ws_plane_i32, 0)
         warm_in = keep.tile([P, 8], F32, name="warm_in")
         warm_out = keep.tile([P, 8], F32, name="warm_out")
         nc.vector.memset(warm_in[:], 0.0)
         nc.scalar.activation(warm_out[:], warm_in[:], RELU)
         nc.vector.tensor_copy(xs_table[0:BLOCKS, :].bitcast(I32), xs_rows[:].bitcast(I32))
-        nc.vector.tensor_copy(ws_plane_i32[0:PACK, :], ws_rows_i32[0:PACK, :])
-        place_scale_rows(nc, ws_plane_i32, ws_rows_i32)
 
         xs_picked = keep.tile([P, S], U8, name="xs_picked", align_bytes=ALIGN)
         nc.vector.tensor_copy(xs_picked[:], xs_table[:].indirect(offsets[:]))
         place_scale_rows(nc, xs_plane[:].bitcast(I32), xs_picked[:].bitcast(I32))
         nc.vector.tensor_copy(xs_plane[0:PACK, :].bitcast(I32), xs_picked[0:PACK, :].bitcast(I32))
+        ws_rows = shared.tile([BLOCKS, 2, N], U8, name="ws_rows", offset=8 * N, align_bytes=ALIGN)
+        for term, scales in enumerate((w1_scales, w3_scales)):
+            nc.sync.dma_start(ws_rows[:, term, :].bitcast(I32), scales[0].bitcast(I32))
+        ws_rows_i32 = ws_rows[:].rearrange("p a n -> p (a n)").bitcast(I32)
         w_words = []
         for term, packed in enumerate((w1_words, w3_words)):
             words = shared.tile([P, N], U32, name="w_words%d" % term, offset=4 * N * term, align_bytes=ALIGN)
             nc.sync.dma_start(words[:].bitcast(I32), words_of(packed))
             w_words.append(words)
+        nc.gpsimd.tensor_copy(ws_plane_i32[0:PACK, :], ws_rows_i32[0:PACK, :])
+        place_scale_rows(nc, ws_plane_i32, ws_rows_i32)
 
         xw_picked = []
         for half in range(2):

@@ -16,27 +16,17 @@ RELU = mybir.ActivationFunctionType.Relu
 
 P = 128
 PACK = 4
-BLOCKS = K // 32
 ALIGN = 64
 HALF = S // 2
 CHUNK = 128
 CHUNKS = S // CHUNK
-PAIR = 2 * CHUNK
-W2_HALF = H // 2
-M_HALF = W2_HALF // PACK
-H_BANKS = 5
-OUT_BANKS = 8 - H_BANKS
-WARM_PASSES = 3
-GROUPS = [(0, 2), (2, 4), (4, 6), (6, 7), (7, 8)]
+WARM_PASSES = 4
+SCALAR_M = 128
+STAGED = slice(32, 96, 4)
 
 
 def words_of(packed):
     return packed[0].rearrange("p n t -> p (n t)").bitcast(I32)
-
-
-def place_scale_rows(nc, plane, rows):
-    for q in range(1, 4):
-        nc.sync.dma_start(plane[32 * q : 32 * q + PACK, :], rows[PACK * q : PACK * (q + 1), :])
 
 
 def tile_picked_lora_relu_p_kernel(
@@ -45,51 +35,45 @@ def tile_picked_lora_relu_p_kernel(
     nc = tc.nc
     with ExitStack() as ctx:
         keep = ctx.enter_context(tc.tile_pool(name="keep", bufs=1))
-        shared = ctx.enter_context(tc.tile_pool(name="shared", bufs=1))
-        h_psum = ctx.enter_context(tc.psum_pool(name="h_psum", bufs=H_BANKS))
-        out_psum = ctx.enter_context(tc.psum_pool(name="out_psum", bufs=OUT_BANKS))
+        psum = ctx.enter_context(tc.psum_pool(name="psum", bufs=1))
 
-        xs_rows = keep.tile([BLOCKS, T], U8, name="xs_rows", align_bytes=ALIGN)
-        nc.scalar.dma_start(xs_rows[:].bitcast(I32), x_scales[0].bitcast(I32))
+        xs_table = keep.tile([P, T], U8, name="xs_table", align_bytes=ALIGN)
+        nc.vector.memset(xs_table[:].bitcast(I32), 0)
+        plane = keep.tile([P, S + 2 * N], U8, name="plane", align_bytes=ALIGN)
+        nc.vector.memset(plane[:].bitcast(I32), 0)
+
         offsets = keep.tile([P, S // 16], U16, name="offsets")
+        w2_raw = keep.tile([P, PACK, H], F32, name="w2_raw")
+        nc.sync.dma_start(w2_raw[:], w2.rearrange("(p j) c -> p j c", j=PACK))
         nc.sync.dma_start(offsets[:], offs)
+        nc.sync.dma_start(xs_table[STAGED, :].bitcast(I32), x_scales[0].bitcast(I32))
+        rows = keep.tile([P, S + 2 * N], U8, name="rows", align_bytes=ALIGN)
+        for term, scales in enumerate((w1_scales, w3_scales)):
+            nc.sync.dma_start(rows[STAGED, S + N * term : S + N * (term + 1)].bitcast(I32), scales[0].bitcast(I32))
         xw_table = keep.tile([P, T], U32, name="xw_table", align_bytes=ALIGN)
         nc.sync.dma_start(xw_table[:].bitcast(I32), words_of(x_words))
-        w2_rows = w2.rearrange("(p j) c -> p j c", j=PACK)
-        w2_raw = []
-        for half in range(2):
-            raw = keep.tile([P, PACK, W2_HALF], F32, name="w2_raw%d" % half)
-            nc.sync.dma_start(raw[:], w2_rows[:, :, W2_HALF * half : W2_HALF * (half + 1)])
-            w2_raw.append(raw)
-
-        xs_table = shared.tile([P, T], U8, name="xs_table", offset=0, align_bytes=ALIGN)
-        nc.vector.memset(xs_table[:].bitcast(I32), 0)
-        xs_plane = keep.tile([P, S], U8, name="xs_plane", align_bytes=ALIGN)
-        nc.vector.memset(xs_plane[:].bitcast(I32), 0)
-        ws_plane = keep.tile([P, 2, N], U8, name="ws_plane", align_bytes=ALIGN)
-        ws_plane_i32 = ws_plane[:].rearrange("p a n -> p (a n)").bitcast(I32)
-        nc.vector.memset(ws_plane_i32, 0)
-        warm_in = keep.tile([P, 8], F32, name="warm_in")
-        warm_out = keep.tile([P, 8], F32, name="warm_out")
-        nc.vector.memset(warm_in[:], 0.0)
-        nc.scalar.activation(warm_out[:], warm_in[:], RELU)
-        nc.vector.tensor_copy(xs_table[0:BLOCKS, :].bitcast(I32), xs_rows[:].bitcast(I32))
+        w_words = []
+        for term, packed in enumerate((w1_words, w3_words)):
+            words = keep.tile([P, N], U32, name="w_words%d" % term, align_bytes=ALIGN)
+            nc.sync.dma_start(words[:].bitcast(I32), words_of(packed))
+            w_words.append(words)
 
         xs_picked = keep.tile([P, S], U8, name="xs_picked", align_bytes=ALIGN)
         nc.vector.tensor_copy(xs_picked[:], xs_table[:].indirect(offsets[:]))
-        place_scale_rows(nc, xs_plane[:].bitcast(I32), xs_picked[:].bitcast(I32))
-        nc.vector.tensor_copy(xs_plane[0:PACK, :].bitcast(I32), xs_picked[0:PACK, :].bitcast(I32))
-        ws_rows = shared.tile([BLOCKS, 2, N], U8, name="ws_rows", offset=8 * N, align_bytes=ALIGN)
-        for term, scales in enumerate((w1_scales, w3_scales)):
-            nc.sync.dma_start(ws_rows[:, term, :].bitcast(I32), scales[0].bitcast(I32))
-        ws_rows_i32 = ws_rows[:].rearrange("p a n -> p (a n)").bitcast(I32)
-        w_words = []
-        for term, packed in enumerate((w1_words, w3_words)):
-            words = shared.tile([P, N], U32, name="w_words%d" % term, offset=4 * N * term, align_bytes=ALIGN)
-            nc.sync.dma_start(words[:].bitcast(I32), words_of(packed))
-            w_words.append(words)
-        nc.gpsimd.tensor_copy(ws_plane_i32[0:PACK, :], ws_rows_i32[0:PACK, :])
-        place_scale_rows(nc, ws_plane_i32, ws_rows_i32)
+        nc.vector.tensor_copy(rows[:, 0:S].bitcast(I32), xs_picked[:].bitcast(I32))
+        for q in range(4):
+            nc.sync.dma_start(plane[32 * q : 32 * q + PACK, :].bitcast(I32), rows[32 + 16 * q : 48 + 16 * q : 4, :].bitcast(I32))
+
+        w2_words = keep.tile([P, H], U32, name="w2_words", align_bytes=ALIGN)
+        w2_plane = keep.tile([P, H], U8, name="w2_plane", align_bytes=ALIGN)
+        w2_bf16 = keep.tile([P, PACK, P, PACK], BF16, name="w2_bf16", align_bytes=ALIGN)
+        source = w2_raw[:].rearrange("p j (m t) -> p m j t", t=PACK)
+        target = w2_bf16[:].rearrange("p t m j -> p m j t")
+        if SCALAR_M > 0:
+            nc.scalar.copy(target[:, 0:SCALAR_M, :, :], source[:, 0:SCALAR_M, :, :])
+        if SCALAR_M < P:
+            nc.vector.tensor_copy(target[:, SCALAR_M:P, :, :], source[:, SCALAR_M:P, :, :])
+        nc.vector.quantize_mx(out=w2_words[:].bitcast(FP8X4), scales=w2_plane[:], in_=w2_bf16[:].rearrange("p t m j -> p (t m j)"))
 
         xw_picked = []
         for half in range(2):
@@ -98,100 +82,133 @@ def tile_picked_lora_relu_p_kernel(
             nc.vector.tensor_copy(picked[:], xw_table[:].indirect(entries))
             xw_picked.append(picked)
 
-        warm_bank = out_psum.tile([P, HALF], F32, name="out_bank")
+        warm_bank = psum.tile([P, HALF], F32, name="bank7")
         for warm_pass in range(WARM_PASSES):
             nc.tensor.matmul_mx(
                 out=warm_bank[:],
-                lhsT=xw_picked[0][:, 0:P].bitcast(FP8X4),
-                lhsT_scale=xs_picked[:, 0:P],
-                rhs=xw_picked[0][:].bitcast(FP8X4),
-                rhs_scale=xs_picked[:, 0:HALF],
+                lhsT=w2_words[:, 0:P].bitcast(FP8X4),
+                lhsT_scale=w2_plane[:, 0:P],
+                rhs=w2_words[:].bitcast(FP8X4),
+                rhs_scale=w2_plane[:],
                 start=True,
                 stop=True,
             )
-
-        w2_words = [keep.tile([P, P], U32, name="w2_words%d" % t, align_bytes=ALIGN) for t in range(PACK)]
-        w2_plane = [keep.tile([P, P], U8, name="w2_plane%d" % t, align_bytes=ALIGN) for t in range(PACK)]
-        w2_bf16 = [keep.tile([P, PACK, M_HALF, PACK], BF16, name="w2_bf16_%d" % half, align_bytes=ALIGN) for half in range(2)]
-
-        def round_w2(half, columns, copy):
-            source = w2_raw[half][:].rearrange("p j (m t) -> p m j t", t=PACK)
-            copy(w2_bf16[half][:].rearrange("p t m j -> p m j t")[:, columns, :, :], source[:, columns, :, :])
-
-        def quantise_w2(half):
-            cols = slice(M_HALF * half, M_HALF * (half + 1))
-            for t in range(PACK):
-                nc.vector.quantize_mx(
-                    out=w2_words[t][:, cols].bitcast(FP8X4),
-                    scales=w2_plane[t][:, cols],
-                    in_=w2_bf16[half][:, t, :, :].rearrange("p m j -> p (m j)"),
-                )
-
-        round_w2(0, slice(0, M_HALF), nc.scalar.copy)
-        round_w2(1, slice(0, M_HALF // 2), nc.scalar.copy)
-        round_w2(1, slice(M_HALF // 2, M_HALF), nc.vector.tensor_copy)
-        quantise_w2(0)
-        quantise_w2(1)
 
         def token_words(c0, c1):
             first = CHUNK * c0 % HALF
             return xw_picked[CHUNK * c0 // HALF][:, first : first + CHUNK * (c1 - c0)].bitcast(FP8X4)
 
-        h_words = [keep.tile([P, PAIR], U32, name="h_words%d" % g, align_bytes=ALIGN) for g in range(S // PAIR)]
-        h_plane = [keep.tile([P, PAIR], U8, name="h_plane%d" % g, align_bytes=ALIGN) for g in range(S // PAIR)]
-        for pair in range(S // PAIR):
-            h_bf16 = []
-            for c in (2 * pair, 2 * pair + 1):
-                h_bank = h_psum.tile([P, PACK, CHUNK], F32, name="h_bank")
-                for t in range(PACK):
-                    nc.tensor.matmul_mx(
-                        out=h_bank[:, t, :],
-                        lhsT=w2_words[t][:].bitcast(FP8X4),
-                        lhsT_scale=w2_plane[t][:],
-                        rhs=token_words(c, c + 1),
-                        rhs_scale=xs_plane[:, CHUNK * c : CHUNK * (c + 1)],
-                        start=True,
-                        stop=True,
-                    )
-                rounded = keep.tile([P, CHUNK, PACK], BF16, name="h_bf16_%d" % c, align_bytes=ALIGN)
-                sums = h_bank[:].rearrange("p t n -> p n t")
-                if c % 2 == 1 and c < CHUNKS - 1:
-                    nc.vector.tensor_scalar_max(rounded[:], sums, 0.0)
-                else:
-                    nc.scalar.activation(rounded[:], sums, RELU)
-                h_bf16.append(rounded)
-            for i in range(2):
-                cols = slice(CHUNK * i, CHUNK * (i + 1))
-                nc.vector.quantize_mx(
-                    out=h_words[pair][:, cols].bitcast(FP8X4),
-                    scales=h_plane[pair][:, cols],
-                    in_=h_bf16[i][:].rearrange("p n t -> p (n t)"),
+        h_words = [keep.tile([P, 2 * CHUNK], U32, name="h_words%d" % g, align_bytes=ALIGN) for g in range(CHUNKS // 2)]
+        h_plane = [keep.tile([P, 2 * CHUNK], U8, name="h_plane%d" % g, align_bytes=ALIGN) for g in range(CHUNKS // 2)]
+        h_banks = {}
+        h_bf16 = {}
+        out_sums = {}
+        out_tiles = out.rearrange("(a p) s -> p a s", p=P)
+
+        def first_product(c, bank):
+            h_bank = psum.tile([P, PACK, CHUNK], F32, name="bank%d" % bank)
+            for t in range(PACK):
+                nc.tensor.matmul_mx(
+                    out=h_bank[:, t, :],
+                    lhsT=w2_words[:, P * t : P * (t + 1)].bitcast(FP8X4),
+                    lhsT_scale=w2_plane[:, P * t : P * (t + 1)],
+                    rhs=token_words(c, c + 1),
+                    rhs_scale=plane[:, CHUNK * c : CHUNK * (c + 1)],
+                    start=True,
+                    stop=True,
+                )
+            h_banks[c] = h_bank
+
+        def relu_round(c, on_scalar):
+            rounded = keep.tile([P, CHUNK, PACK], BF16, name="h_bf16_%d" % c, align_bytes=ALIGN)
+            sums = h_banks[c][:].rearrange("p t n -> p n t")
+            if on_scalar:
+                nc.scalar.activation(rounded[:], sums, RELU)
+            else:
+                nc.vector.tensor_scalar_max(rounded[:], sums, 0.0)
+            h_bf16[c] = rounded
+
+        def quantise(c):
+            cols = slice(CHUNK * (c % 2), CHUNK * (c % 2 + 1))
+            nc.vector.quantize_mx(
+                out=h_words[c // 2][:, cols].bitcast(FP8X4),
+                scales=h_plane[c // 2][:, cols],
+                in_=h_bf16[c][:].rearrange("p n t -> p (n t)"),
+            )
+
+        def term_passes(c0, c1, term, bank=None):
+            width = CHUNK * (c1 - c0)
+            if term == 0:
+                out_bank = psum.tile([P, HALF], F32, name="bank%d" % bank)
+                out_sums[c0] = out_bank[:, 0 : 2 * width].rearrange("p (a s) -> p a s", a=2)
+                words, scales = token_words(c0, c1), plane[:, CHUNK * c0 : CHUNK * c1]
+            else:
+                h_cols = slice(CHUNK * (c0 % 2), CHUNK * (c0 % 2) + width)
+                words, scales = h_words[c0 // 2][:, h_cols].bitcast(FP8X4), h_plane[c0 // 2][:, h_cols]
+            for a in range(2):
+                nc.tensor.matmul_mx(
+                    out=out_sums[c0][:, a, :],
+                    lhsT=w_words[term][:, P * a : P * (a + 1)].bitcast(FP8X4),
+                    lhsT_scale=plane[:, S + N * term + P * a : S + N * term + P * (a + 1)],
+                    rhs=words,
+                    rhs_scale=scales,
+                    start=(term == 0 and a == 0),
+                    stop=(term == 1 and a == 1),
                 )
 
-        out_tiles = out.rearrange("(a p) s -> p a s", p=P)
-        for g, (c0, c1) in enumerate(GROUPS):
-            width = CHUNK * (c1 - c0)
-            out_bank = out_psum.tile([P, HALF], F32, name="out_bank")
-            sums = out_bank[:, 0 : 2 * width].rearrange("p (a s) -> p a s", a=2)
-            h_cols = slice(CHUNK * (c0 % 2), CHUNK * (c0 % 2) + width)
-            moving = (
-                (token_words(c0, c1), xs_plane[:, CHUNK * c0 : CHUNK * c1]),
-                (h_words[c0 // 2][:, h_cols].bitcast(FP8X4), h_plane[c0 // 2][:, h_cols]),
-            )
-            for term, (words, plane) in enumerate(moving):
-                for a in range(2):
-                    nc.tensor.matmul_mx(
-                        out=sums[:, a, :],
-                        lhsT=w_words[term][:, P * a : P * (a + 1)].bitcast(FP8X4),
-                        lhsT_scale=ws_plane[:, term, P * a : P * (a + 1)],
-                        rhs=words,
-                        rhs_scale=plane,
-                        start=(term == 0 and a == 0),
-                        stop=(term == 1 and a == 1),
-                    )
-            result = keep.tile([P, 2, width], F32, name="result%d" % g)
-            if g >= 2 and g % 2 == 0:
-                nc.vector.tensor_copy(result[:], sums)
+        def store(c0, c1, on_scalar):
+            result = keep.tile([P, 2, CHUNK * (c1 - c0)], F32, name="result%d" % c0)
+            if on_scalar:
+                nc.scalar.copy(result[:], out_sums[c0])
             else:
-                nc.scalar.copy(result[:], sums)
+                nc.vector.tensor_copy(result[:], out_sums[c0])
             nc.sync.dma_start(out_tiles[:, :, CHUNK * c0 : CHUNK * c1], result[:])
+
+        first_product(0, 0)
+        first_product(1, 1)
+        first_product(2, 2)
+        first_product(3, 3)
+        relu_round(0, True)
+        relu_round(1, True)
+        relu_round(2, False)
+        quantise(0)
+        quantise(1)
+        relu_round(3, True)
+        term_passes(0, 1, 0, 6)
+        first_product(4, 4)
+        first_product(5, 5)
+        first_product(6, 0)
+        first_product(7, 1)
+        term_passes(0, 1, 1)
+        term_passes(1, 2, 0, 7)
+        term_passes(1, 2, 1)
+        relu_round(4, False)
+        relu_round(5, True)
+        quantise(2)
+        quantise(3)
+        term_passes(2, 3, 0, 2)
+        term_passes(2, 3, 1)
+        term_passes(3, 4, 0, 3)
+        term_passes(3, 4, 1)
+        quantise(4)
+        store(0, 1, False)
+        relu_round(6, True)
+        term_passes(4, 5, 0, 4)
+        term_passes(4, 5, 1)
+        quantise(5)
+        quantise(6)
+        store(1, 2, False)
+        term_passes(5, 6, 0, 5)
+        term_passes(5, 6, 1)
+        relu_round(7, True)
+        term_passes(6, 7, 0, 0)
+        term_passes(6, 7, 1)
+        quantise(7)
+        store(2, 3, True)
+        term_passes(7, 8, 0, 6)
+        term_passes(7, 8, 1)
+        store(3, 4, False)
+        store(4, 5, True)
+        store(5, 6, False)
+        store(6, 7, True)
+        store(7, 8, False)

@@ -20,7 +20,7 @@ ALIGN = 64
 HALF = S // 2
 CHUNK = 128
 CHUNKS = S // CHUNK
-WARM_PASSES = 4
+WARM_PASSES = 3
 SCALAR_M = 128
 STAGED = slice(32, 96, 4)
 
@@ -62,7 +62,7 @@ def tile_picked_lora_relu_p_kernel(
         nc.vector.tensor_copy(xs_picked[:], xs_table[:].indirect(offsets[:]))
         nc.vector.tensor_copy(rows[:, 0:S].bitcast(I32), xs_picked[:].bitcast(I32))
         for q in range(4):
-            nc.sync.dma_start(plane[32 * q : 32 * q + PACK, :].bitcast(I32), rows[32 + 16 * q : 48 + 16 * q : 4, :].bitcast(I32))
+            nc.scalar.dma_start(plane[32 * q : 32 * q + PACK, :].bitcast(I32), rows[32 + 16 * q : 48 + 16 * q : 4, :].bitcast(I32))
 
         w2_words = keep.tile([P, H], U32, name="w2_words", align_bytes=ALIGN)
         w2_plane = keep.tile([P, H], U8, name="w2_plane", align_bytes=ALIGN)
@@ -101,7 +101,7 @@ def tile_picked_lora_relu_p_kernel(
         h_words = [keep.tile([P, 2 * CHUNK], U32, name="h_words%d" % g, align_bytes=ALIGN) for g in range(CHUNKS // 2)]
         h_plane = [keep.tile([P, 2 * CHUNK], U8, name="h_plane%d" % g, align_bytes=ALIGN) for g in range(CHUNKS // 2)]
         h_banks = {}
-        h_bf16 = {}
+        h_bf16 = [keep.tile([P, 2 * CHUNK, PACK], BF16, name="h_bf16_%d" % g, align_bytes=ALIGN) for g in range(CHUNKS // 2)]
         out_sums = {}
         out_tiles = out.rearrange("(a p) s -> p a s", p=P)
 
@@ -120,95 +120,94 @@ def tile_picked_lora_relu_p_kernel(
             h_banks[c] = h_bank
 
         def relu_round(c, on_scalar):
-            rounded = keep.tile([P, CHUNK, PACK], BF16, name="h_bf16_%d" % c, align_bytes=ALIGN)
+            rounded = h_bf16[c // 2][:, CHUNK * (c % 2) : CHUNK * (c % 2 + 1), :]
             sums = h_banks[c][:].rearrange("p t n -> p n t")
             if on_scalar:
-                nc.scalar.activation(rounded[:], sums, RELU)
+                nc.scalar.activation(rounded, sums, RELU)
             else:
-                nc.vector.tensor_scalar_max(rounded[:], sums, 0.0)
-            h_bf16[c] = rounded
+                nc.vector.tensor_scalar_max(rounded, sums, 0.0)
 
-        def quantise(c):
-            cols = slice(CHUNK * (c % 2), CHUNK * (c % 2 + 1))
+        def quantise(c0, c1):
+            cols = slice(CHUNK * (c0 % 2), CHUNK * (c0 % 2 + c1 - c0))
             nc.vector.quantize_mx(
-                out=h_words[c // 2][:, cols].bitcast(FP8X4),
-                scales=h_plane[c // 2][:, cols],
-                in_=h_bf16[c][:].rearrange("p n t -> p (n t)"),
+                out=h_words[c0 // 2][:, cols].bitcast(FP8X4),
+                scales=h_plane[c0 // 2][:, cols],
+                in_=h_bf16[c0 // 2][:, cols, :].rearrange("p n t -> p (n t)"),
             )
 
-        def term_passes(c0, c1, term, bank=None):
+        def term_passes(c0, c1, tiles, term, bank=None):
             width = CHUNK * (c1 - c0)
             if term == 0:
                 out_bank = psum.tile([P, HALF], F32, name="bank%d" % bank)
-                out_sums[c0] = out_bank[:, 0 : 2 * width].rearrange("p (a s) -> p a s", a=2)
+                out_sums[c0, tiles] = out_bank[:, 0 : len(tiles) * width].rearrange("p (a s) -> p a s", a=len(tiles))
                 words, scales = token_words(c0, c1), plane[:, CHUNK * c0 : CHUNK * c1]
             else:
                 h_cols = slice(CHUNK * (c0 % 2), CHUNK * (c0 % 2) + width)
                 words, scales = h_words[c0 // 2][:, h_cols].bitcast(FP8X4), h_plane[c0 // 2][:, h_cols]
-            for a in range(2):
+            for i, a in enumerate(tiles):
                 nc.tensor.matmul_mx(
-                    out=out_sums[c0][:, a, :],
+                    out=out_sums[c0, tiles][:, i, :],
                     lhsT=w_words[term][:, P * a : P * (a + 1)].bitcast(FP8X4),
                     lhsT_scale=plane[:, S + N * term + P * a : S + N * term + P * (a + 1)],
                     rhs=words,
                     rhs_scale=scales,
-                    start=(term == 0 and a == 0),
-                    stop=(term == 1 and a == 1),
+                    start=(term == 0 and i == 0),
+                    stop=(term == 1 and i == len(tiles) - 1),
                 )
 
-        def store(c0, c1, on_scalar):
-            result = keep.tile([P, 2, CHUNK * (c1 - c0)], F32, name="result%d" % c0)
+        def store(c0, c1, tiles, on_scalar, queue=nc.sync):
+            result = keep.tile([P, len(tiles), CHUNK * (c1 - c0)], F32, name="result%d_%d" % (c0, tiles[0]))
             if on_scalar:
-                nc.scalar.copy(result[:], out_sums[c0])
+                nc.scalar.copy(result[:], out_sums[c0, tiles])
             else:
-                nc.vector.tensor_copy(result[:], out_sums[c0])
-            nc.sync.dma_start(out_tiles[:, :, CHUNK * c0 : CHUNK * c1], result[:])
+                nc.vector.tensor_copy(result[:], out_sums[c0, tiles])
+            queue.dma_start(out_tiles[:, tiles[0] : tiles[-1] + 1, CHUNK * c0 : CHUNK * c1], result[:])
 
         first_product(0, 0)
         first_product(1, 1)
         first_product(2, 2)
         first_product(3, 3)
         relu_round(0, True)
-        relu_round(1, True)
-        relu_round(2, False)
-        quantise(0)
-        quantise(1)
+        relu_round(1, False)
+        relu_round(2, True)
+        quantise(0, 1)
+        quantise(1, 2)
         relu_round(3, True)
-        term_passes(0, 1, 0, 6)
         first_product(4, 4)
         first_product(5, 5)
+        term_passes(0, 2, (0,), 0, 6)
+        term_passes(0, 2, (1,), 0, 7)
         first_product(6, 0)
+        term_passes(0, 2, (0,), 1)
+        term_passes(0, 2, (1,), 1)
         first_product(7, 1)
-        term_passes(0, 1, 1)
-        term_passes(1, 2, 0, 7)
-        term_passes(1, 2, 1)
+        quantise(2, 3)
         relu_round(4, False)
         relu_round(5, True)
-        quantise(2)
-        quantise(3)
-        term_passes(2, 3, 0, 2)
-        term_passes(2, 3, 1)
-        term_passes(3, 4, 0, 3)
-        term_passes(3, 4, 1)
-        quantise(4)
-        store(0, 1, False)
-        relu_round(6, True)
-        term_passes(4, 5, 0, 4)
-        term_passes(4, 5, 1)
-        quantise(5)
-        quantise(6)
-        store(1, 2, False)
-        term_passes(5, 6, 0, 5)
-        term_passes(5, 6, 1)
+        quantise(3, 4)
+        term_passes(2, 4, (0,), 0, 2)
+        term_passes(2, 4, (1,), 0, 3)
+        term_passes(2, 4, (0,), 1)
+        term_passes(2, 4, (1,), 1)
+        store(0, 2, (0,), True)
+        quantise(4, 5)
+        quantise(5, 6)
+        store(0, 2, (1,), False)
         relu_round(7, True)
-        term_passes(6, 7, 0, 0)
-        term_passes(6, 7, 1)
-        quantise(7)
-        store(2, 3, True)
-        term_passes(7, 8, 0, 6)
-        term_passes(7, 8, 1)
-        store(3, 4, False)
-        store(4, 5, True)
-        store(5, 6, False)
-        store(6, 7, True)
-        store(7, 8, False)
+        relu_round(6, False)
+        term_passes(4, 6, (0,), 0, 4)
+        term_passes(4, 6, (1,), 0, 5)
+        term_passes(4, 6, (0,), 1)
+        term_passes(4, 6, (1,), 1)
+        store(2, 4, (0,), True)
+        store(2, 4, (1,), True)
+        term_passes(6, 8, (0,), 0, 6)
+        term_passes(6, 8, (1,), 0, 7)
+        quantise(7, 8)
+        quantise(6, 7)
+        term_passes(6, 8, (0,), 1)
+        term_passes(6, 8, (1,), 1)
+        store(4, 6, (0,), True)
+        store(4, 6, (1,), False)
+        store(6, 8, (0,), False)
+        store(6, 8, (1,), True, nc.scalar)

@@ -46,10 +46,10 @@ def tile_picked_lora_relu_p_kernel(
         w2_raw = keep.tile([P, PACK, H], F32, name="w2_raw")
         nc.sync.dma_start(w2_raw[:], w2.rearrange("(p j) c -> p j c", j=PACK))
         nc.sync.dma_start(offsets[:], offs)
-        nc.sync.dma_start(xs_table[STAGED, :].bitcast(I32), x_scales[0].bitcast(I32))
         rows = keep.tile([P, S + 2 * N], U8, name="rows", align_bytes=ALIGN)
         for term, scales in enumerate((w1_scales, w3_scales)):
             nc.sync.dma_start(rows[STAGED, S + N * term : S + N * (term + 1)].bitcast(I32), scales[0].bitcast(I32))
+        nc.sync.dma_start(xs_table[STAGED, :].bitcast(I32), x_scales[0].bitcast(I32))
         xw_table = keep.tile([P, T], U32, name="xw_table", align_bytes=ALIGN)
         nc.sync.dma_start(xw_table[:].bitcast(I32), words_of(x_words))
         w_words = []
@@ -61,8 +61,8 @@ def tile_picked_lora_relu_p_kernel(
         xs_picked = keep.tile([P, S], U8, name="xs_picked", align_bytes=ALIGN)
         nc.vector.tensor_copy(xs_picked[:], xs_table[:].indirect(offsets[:]))
         nc.vector.tensor_copy(rows[:, 0:S].bitcast(I32), xs_picked[:].bitcast(I32))
-        for q in range(4):
-            nc.scalar.dma_start(plane[32 * q : 32 * q + PACK, :].bitcast(I32), rows[32 + 16 * q : 48 + 16 * q : 4, :].bitcast(I32))
+        for r in range(PACK):
+            nc.scalar.dma_start(plane[r:P:32, :].bitcast(I32), rows[32 + 4 * r : 96 : 16, :].bitcast(I32))
 
         w2_words = keep.tile([P, H], U32, name="w2_words", align_bytes=ALIGN)
         w2_plane = keep.tile([P, H], U8, name="w2_plane", align_bytes=ALIGN)

@@ -17,12 +17,15 @@ RELU = mybir.ActivationFunctionType.Relu
 P = 128
 PACK = 4
 ALIGN = 64
+BANKS = 8
+BANK = 512
 HALF = S // 2
 CHUNK = 128
-CHUNKS = S // CHUNK
-WARM_PASSES = 3
-SCALAR_M = 128
+PAIR = 2 * CHUNK
+PAIRS = S // PAIR
+ROW_TILES = N // P
 STAGED = slice(32, 96, 4)
+WARM_PASSES = 4
 
 
 def words_of(packed):
@@ -39,16 +42,17 @@ def tile_picked_lora_relu_p_kernel(
 
         xs_table = keep.tile([P, T], U8, name="xs_table", align_bytes=ALIGN)
         nc.vector.memset(xs_table[:].bitcast(I32), 0)
-        plane = keep.tile([P, S + 2 * N], U8, name="plane", align_bytes=ALIGN)
-        nc.vector.memset(plane[:].bitcast(I32), 0)
+        scale_plane = keep.tile([P, S + 2 * N], U8, name="scale_plane", align_bytes=ALIGN)
+        nc.vector.memset(scale_plane[:].bitcast(I32), 0)
 
-        offsets = keep.tile([P, S // 16], U16, name="offsets")
         w2_raw = keep.tile([P, PACK, H], F32, name="w2_raw")
         nc.sync.dma_start(w2_raw[:], w2.rearrange("(p j) c -> p j c", j=PACK))
+        offsets = keep.tile([P, S // 16], U16, name="offsets")
         nc.sync.dma_start(offsets[:], offs)
-        rows = keep.tile([P, S + 2 * N], U8, name="rows", align_bytes=ALIGN)
+        scale_rows = keep.tile([P, S + 2 * N], U8, name="scale_rows", align_bytes=ALIGN)
         for term, scales in enumerate((w1_scales, w3_scales)):
-            nc.sync.dma_start(rows[STAGED, S + N * term : S + N * (term + 1)].bitcast(I32), scales[0].bitcast(I32))
+            cols = slice(S + N * term, S + N * (term + 1))
+            nc.sync.dma_start(scale_rows[STAGED, cols].bitcast(I32), scales[0].bitcast(I32))
         nc.sync.dma_start(xs_table[STAGED, :].bitcast(I32), x_scales[0].bitcast(I32))
         xw_table = keep.tile([P, T], U32, name="xw_table", align_bytes=ALIGN)
         nc.sync.dma_start(xw_table[:].bitcast(I32), words_of(x_words))
@@ -60,20 +64,19 @@ def tile_picked_lora_relu_p_kernel(
 
         xs_picked = keep.tile([P, S], U8, name="xs_picked", align_bytes=ALIGN)
         nc.vector.tensor_copy(xs_picked[:], xs_table[:].indirect(offsets[:]))
-        nc.vector.tensor_copy(rows[:, 0:S].bitcast(I32), xs_picked[:].bitcast(I32))
+        nc.vector.tensor_copy(scale_rows[:, 0:S].bitcast(I32), xs_picked[:].bitcast(I32))
         for r in range(PACK):
-            nc.scalar.dma_start(plane[r:P:32, :].bitcast(I32), rows[32 + 4 * r : 96 : 16, :].bitcast(I32))
+            nc.scalar.dma_start(scale_plane[r:P:32, :].bitcast(I32), scale_rows[32 + 4 * r : 96 : 16, :].bitcast(I32))
 
+        w2_bf16 = keep.tile([P, PACK, P, PACK], BF16, name="w2_bf16", align_bytes=ALIGN)
+        nc.scalar.copy(w2_bf16[:].rearrange("p t m j -> p m j t"), w2_raw[:].rearrange("p j (m t) -> p m j t", t=PACK))
         w2_words = keep.tile([P, H], U32, name="w2_words", align_bytes=ALIGN)
         w2_plane = keep.tile([P, H], U8, name="w2_plane", align_bytes=ALIGN)
-        w2_bf16 = keep.tile([P, PACK, P, PACK], BF16, name="w2_bf16", align_bytes=ALIGN)
-        source = w2_raw[:].rearrange("p j (m t) -> p m j t", t=PACK)
-        target = w2_bf16[:].rearrange("p t m j -> p m j t")
-        if SCALAR_M > 0:
-            nc.scalar.copy(target[:, 0:SCALAR_M, :, :], source[:, 0:SCALAR_M, :, :])
-        if SCALAR_M < P:
-            nc.vector.tensor_copy(target[:, SCALAR_M:P, :, :], source[:, SCALAR_M:P, :, :])
-        nc.vector.quantize_mx(out=w2_words[:].bitcast(FP8X4), scales=w2_plane[:], in_=w2_bf16[:].rearrange("p t m j -> p (t m j)"))
+        nc.vector.quantize_mx(
+            out=w2_words[:].bitcast(FP8X4),
+            scales=w2_plane[:],
+            in_=w2_bf16[:].rearrange("p t m j -> p (t m j)"),
+        )
 
         xw_picked = []
         for half in range(2):
@@ -82,7 +85,7 @@ def tile_picked_lora_relu_p_kernel(
             nc.vector.tensor_copy(picked[:], xw_table[:].indirect(entries))
             xw_picked.append(picked)
 
-        warm_bank = psum.tile([P, HALF], F32, name="bank7")
+        warm_bank = psum.tile([P, BANK], F32, name="bank%d" % (BANKS - 1))
         for warm_pass in range(WARM_PASSES):
             nc.tensor.matmul_mx(
                 out=warm_bank[:],
@@ -94,120 +97,95 @@ def tile_picked_lora_relu_p_kernel(
                 stop=True,
             )
 
-        def token_words(c0, c1):
-            first = CHUNK * c0 % HALF
-            return xw_picked[CHUNK * c0 // HALF][:, first : first + CHUNK * (c1 - c0)].bitcast(FP8X4)
+        taken = []
 
-        h_words = [keep.tile([P, 2 * CHUNK], U32, name="h_words%d" % g, align_bytes=ALIGN) for g in range(CHUNKS // 2)]
-        h_plane = [keep.tile([P, 2 * CHUNK], U8, name="h_plane%d" % g, align_bytes=ALIGN) for g in range(CHUNKS // 2)]
-        h_banks = {}
-        h_bf16 = [keep.tile([P, 2 * CHUNK, PACK], BF16, name="h_bf16_%d" % g, align_bytes=ALIGN) for g in range(CHUNKS // 2)]
-        out_sums = {}
+        def take_bank():
+            taken.append(psum.tile([P, BANK], F32, name="bank%d" % (len(taken) % BANKS)))
+            return taken[-1]
+
+        def tokens(first, width):
+            start = first % HALF
+            words = xw_picked[first // HALF][:, start : start + width].bitcast(FP8X4)
+            return words, scale_plane[:, first : first + width]
+
+        h_bf16 = [keep.tile([P, PAIR, PACK], BF16, name="h_bf16_%d" % g, align_bytes=ALIGN) for g in range(PAIRS)]
+        h_words = [keep.tile([P, PAIR], U32, name="h_words%d" % g, align_bytes=ALIGN) for g in range(PAIRS)]
+        h_plane = [keep.tile([P, PAIR], U8, name="h_plane%d" % g, align_bytes=ALIGN) for g in range(PAIRS)]
         out_tiles = out.rearrange("(a p) s -> p a s", p=P)
 
-        def first_product(c, bank):
-            h_bank = psum.tile([P, PACK, CHUNK], F32, name="bank%d" % bank)
+        def first_product(c):
+            sums = take_bank()[:].rearrange("p (t n) -> p t n", t=PACK)
+            words, scales = tokens(CHUNK * c, CHUNK)
             for t in range(PACK):
                 nc.tensor.matmul_mx(
-                    out=h_bank[:, t, :],
+                    out=sums[:, t, :],
                     lhsT=w2_words[:, P * t : P * (t + 1)].bitcast(FP8X4),
                     lhsT_scale=w2_plane[:, P * t : P * (t + 1)],
-                    rhs=token_words(c, c + 1),
-                    rhs_scale=plane[:, CHUNK * c : CHUNK * (c + 1)],
+                    rhs=words,
+                    rhs_scale=scales,
                     start=True,
                     stop=True,
                 )
-            h_banks[c] = h_bank
+            return sums
 
-        def relu_round(c, on_scalar):
-            rounded = h_bf16[c // 2][:, CHUNK * (c % 2) : CHUNK * (c % 2 + 1), :]
-            sums = h_banks[c][:].rearrange("p t n -> p n t")
+        def in_pair(c):
+            return slice(CHUNK * (c % 2), CHUNK * (c % 2 + 1))
+
+        def relu_round(c, sums, on_scalar):
+            rounded = h_bf16[c // 2][:, in_pair(c), :]
             if on_scalar:
-                nc.scalar.activation(rounded, sums, RELU)
+                nc.scalar.activation(rounded, sums.rearrange("p t n -> p n t"), RELU)
             else:
-                nc.vector.tensor_scalar_max(rounded, sums, 0.0)
+                nc.vector.tensor_scalar_max(rounded, sums.rearrange("p t n -> p n t"), 0.0)
 
-        def quantise(c0, c1):
-            cols = slice(CHUNK * (c0 % 2), CHUNK * (c0 % 2 + c1 - c0))
+        def quantise_h(c):
             nc.vector.quantize_mx(
-                out=h_words[c0 // 2][:, cols].bitcast(FP8X4),
-                scales=h_plane[c0 // 2][:, cols],
-                in_=h_bf16[c0 // 2][:, cols, :].rearrange("p n t -> p (n t)"),
+                out=h_words[c // 2][:, in_pair(c)].bitcast(FP8X4),
+                scales=h_plane[c // 2][:, in_pair(c)],
+                in_=h_bf16[c // 2][:, in_pair(c), :].rearrange("p n t -> p (n t)"),
             )
 
-        def term_passes(c0, c1, tiles, term, bank=None):
-            width = CHUNK * (c1 - c0)
-            if term == 0:
-                out_bank = psum.tile([P, HALF], F32, name="bank%d" % bank)
-                out_sums[c0, tiles] = out_bank[:, 0 : len(tiles) * width].rearrange("p (a s) -> p a s", a=len(tiles))
-                words, scales = token_words(c0, c1), plane[:, CHUNK * c0 : CHUNK * c1]
-            else:
-                h_cols = slice(CHUNK * (c0 % 2), CHUNK * (c0 % 2) + width)
-                words, scales = h_words[c0 // 2][:, h_cols].bitcast(FP8X4), h_plane[c0 // 2][:, h_cols]
-            for i, a in enumerate(tiles):
-                nc.tensor.matmul_mx(
-                    out=out_sums[c0, tiles][:, i, :],
-                    lhsT=w_words[term][:, P * a : P * (a + 1)].bitcast(FP8X4),
-                    lhsT_scale=plane[:, S + N * term + P * a : S + N * term + P * (a + 1)],
-                    rhs=words,
-                    rhs_scale=scales,
-                    start=(term == 0 and i == 0),
-                    stop=(term == 1 and i == len(tiles) - 1),
-                )
+        def add_term(sums, term, a, words, scales):
+            first = S + N * term + P * a
+            nc.tensor.matmul_mx(
+                out=sums,
+                lhsT=w_words[term][:, P * a : P * (a + 1)].bitcast(FP8X4),
+                lhsT_scale=scale_plane[:, first : first + P],
+                rhs=words,
+                rhs_scale=scales,
+                start=(term == 0),
+                stop=(term == 1),
+            )
 
-        def store(c0, c1, tiles, on_scalar, queue=nc.sync):
-            result = keep.tile([P, len(tiles), CHUNK * (c1 - c0)], F32, name="result%d_%d" % (c0, tiles[0]))
-            if on_scalar:
-                nc.scalar.copy(result[:], out_sums[c0, tiles])
-            else:
-                nc.vector.tensor_copy(result[:], out_sums[c0, tiles])
-            queue.dma_start(out_tiles[:, tiles[0] : tiles[-1] + 1, CHUNK * c0 : CHUNK * c1], result[:])
+        def open_groups(g):
+            groups = [take_bank()[:, 0:PAIR] for a in range(ROW_TILES)]
+            for a, sums in enumerate(groups):
+                add_term(sums, 0, a, *tokens(PAIR * g, PAIR))
+            return groups
 
-        first_product(0, 0)
-        first_product(1, 1)
-        first_product(2, 2)
-        first_product(3, 3)
-        relu_round(0, True)
-        relu_round(1, False)
-        relu_round(2, True)
-        quantise(0, 1)
-        quantise(1, 2)
-        relu_round(3, True)
-        first_product(4, 4)
-        first_product(5, 5)
-        term_passes(0, 2, (0,), 0, 6)
-        term_passes(0, 2, (1,), 0, 7)
-        first_product(6, 0)
-        term_passes(0, 2, (0,), 1)
-        term_passes(0, 2, (1,), 1)
-        first_product(7, 1)
-        quantise(2, 3)
-        relu_round(4, False)
-        relu_round(5, True)
-        quantise(3, 4)
-        term_passes(2, 4, (0,), 0, 2)
-        term_passes(2, 4, (1,), 0, 3)
-        term_passes(2, 4, (0,), 1)
-        term_passes(2, 4, (1,), 1)
-        store(0, 2, (0,), True)
-        quantise(4, 5)
-        quantise(5, 6)
-        store(0, 2, (1,), False)
-        relu_round(7, True)
-        relu_round(6, False)
-        term_passes(4, 6, (0,), 0, 4)
-        term_passes(4, 6, (1,), 0, 5)
-        term_passes(4, 6, (0,), 1)
-        term_passes(4, 6, (1,), 1)
-        store(2, 4, (0,), True)
-        store(2, 4, (1,), True)
-        term_passes(6, 8, (0,), 0, 6)
-        term_passes(6, 8, (1,), 0, 7)
-        quantise(7, 8)
-        quantise(6, 7)
-        term_passes(6, 8, (0,), 1)
-        term_passes(6, 8, (1,), 1)
-        store(4, 6, (0,), True)
-        store(4, 6, (1,), False)
-        store(6, 8, (0,), False)
-        store(6, 8, (1,), True, nc.scalar)
+        def close_groups(g, groups):
+            for a, sums in enumerate(groups):
+                add_term(sums, 1, a, h_words[g][:].bitcast(FP8X4), h_plane[g][:])
+
+        def store(g, a, sums, copy, queue):
+            result = keep.tile([P, PAIR], F32, name="result%d_%d" % (g, a))
+            copy(result[:], sums)
+            queue.dma_start(out_tiles[:, a, PAIR * g : PAIR * (g + 1)], result[:])
+
+        vector_chunks = (1, 4, 6)
+        for g in range(PAIRS + 2):
+            if g < PAIRS:
+                chunks = (2 * g, 2 * g + 1)
+                h_sums = [first_product(c) for c in chunks]
+                for c, sums in zip(chunks, h_sums):
+                    relu_round(c, sums, on_scalar=c not in vector_chunks)
+                for c in chunks:
+                    quantise_h(c)
+            if g >= 2:
+                done = g - 2
+                groups = open_groups(done)
+                close_groups(done, groups)
+                last = done == PAIRS - 1
+                copies = {0: (nc.scalar.copy, nc.vector.tensor_copy), 1: (nc.scalar.copy, nc.scalar.copy), 2: (nc.scalar.copy, nc.vector.tensor_copy), 3: (nc.vector.tensor_copy, nc.scalar.copy)}[done]
+                for a in range(ROW_TILES):
+                    store(done, a, groups[a], copies[a], nc.scalar if last and a == 1 else nc.sync)

@@ -21,11 +21,14 @@ BANKS = 8
 BANK = 512
 HALF = S // 2
 CHUNK = 128
+CHUNKS = S // CHUNK
 PAIR = 2 * CHUNK
 PAIRS = S // PAIR
 ROW_TILES = N // P
 STAGED = slice(32, 96, 4)
-WARM_PASSES = 4
+AHEAD = 4
+LAG = 3
+WARM_PASSES = 3
 
 
 def words_of(packed):
@@ -172,20 +175,26 @@ def tile_picked_lora_relu_p_kernel(
             copy(result[:], sums)
             queue.dma_start(out_tiles[:, a, PAIR * g : PAIR * (g + 1)], result[:])
 
-        vector_chunks = (1, 4, 6)
-        for g in range(PAIRS + 2):
-            if g < PAIRS:
-                chunks = (2 * g, 2 * g + 1)
-                h_sums = [first_product(c) for c in chunks]
-                for c, sums in zip(chunks, h_sums):
-                    relu_round(c, sums, on_scalar=c not in vector_chunks)
-                for c in chunks:
-                    quantise_h(c)
-            if g >= 2:
-                done = g - 2
-                groups = open_groups(done)
-                close_groups(done, groups)
-                last = done == PAIRS - 1
-                copies = {0: (nc.scalar.copy, nc.vector.tensor_copy), 1: (nc.scalar.copy, nc.scalar.copy), 2: (nc.scalar.copy, nc.vector.tensor_copy), 3: (nc.vector.tensor_copy, nc.scalar.copy)}[done]
+        def on_vector(i):
+            return i % 3 == 1
+
+        h_sums = [first_product(c) for c in range(AHEAD)]
+        groups = []
+        for c in range(CHUNKS + 1 + LAG):
+            if c < CHUNKS:
+                relu_round(c, h_sums[c], on_scalar=not on_vector(c))
+            if 1 <= c <= CHUNKS:
+                quantise_h(c - 1)
+            if 2 <= c <= CHUNKS and c % 2 == 0:
+                close_groups(c // 2 - 1, groups[-1])
+            if c + AHEAD < CHUNKS:
+                h_sums.append(first_product(c + AHEAD))
+            if c < CHUNKS and c % 2 == 1:
+                groups.append(open_groups(c // 2))
+            if c - LAG >= 2 and (c - LAG) % 2 == 0:
+                g = (c - LAG) // 2 - 1
                 for a in range(ROW_TILES):
-                    store(done, a, groups[a], copies[a], nc.scalar if last and a == 1 else nc.sync)
+                    if on_vector(ROW_TILES * g + a):
+                        store(g, a, groups[g][a], nc.vector.tensor_copy, nc.sync)
+                    else:
+                        store(g, a, groups[g][a], nc.scalar.copy, nc.scalar if g == PAIRS - 1 else nc.sync)

@@ -148,7 +148,7 @@ def tile_picked_lora_relu_p_kernel(
                 in_=h_bf16[c // 2][:, in_pair(c), :].rearrange("p n t -> p (n t)"),
             )
 
-        def add_term(sums, term, a, words, scales):
+        def add_term(sums, term, a, words, scales, stop=False):
             first = S + N * term + P * a
             nc.tensor.matmul_mx(
                 out=sums,
@@ -157,7 +157,7 @@ def tile_picked_lora_relu_p_kernel(
                 rhs=words,
                 rhs_scale=scales,
                 start=(term == 0),
-                stop=(term == 1),
+                stop=stop,
             )
 
         def open_groups(g):
@@ -167,8 +167,10 @@ def tile_picked_lora_relu_p_kernel(
             return groups
 
         def close_groups(g, groups):
-            for a, sums in enumerate(groups):
-                add_term(sums, 1, a, h_words[g][:].bitcast(FP8X4), h_plane[g][:])
+            parts = [in_pair(0), in_pair(1)] if g == PAIRS - 1 else [slice(0, PAIR)]
+            for cols in parts:
+                for a, sums in enumerate(groups):
+                    add_term(sums[:, cols], 1, a, h_words[g][:, cols].bitcast(FP8X4), h_plane[g][:, cols], cols.stop == PAIR)
 
         def store(g, a, sums, copy, queue):
             result = keep.tile([P, PAIR], F32, name="result%d_%d" % (g, a))
@@ -193,8 +195,10 @@ def tile_picked_lora_relu_p_kernel(
                 groups.append(open_groups(c // 2))
             if c - LAG >= 2 and (c - LAG) % 2 == 0:
                 g = (c - LAG) // 2 - 1
-                for a in range(ROW_TILES):
-                    if on_vector(ROW_TILES * g + a):
-                        store(g, a, groups[g][a], nc.vector.tensor_copy, nc.sync)
-                    else:
-                        store(g, a, groups[g][a], nc.scalar.copy, nc.scalar if g == PAIRS - 1 else nc.sync)
+                if g < PAIRS - 1:
+                    for a in range(ROW_TILES):
+                        copy = nc.vector.tensor_copy if on_vector(ROW_TILES * g + a) else nc.scalar.copy
+                        store(g, a, groups[g][a], copy, nc.sync)
+                else:
+                    store(g, 0, groups[g][0], nc.vector.tensor_copy, nc.sync)
+                    store(g, 1, groups[g][1], nc.scalar.copy, nc.scalar)

@@ -55,7 +55,7 @@ def tile_picked_lora_relu_p_kernel(
         scale_rows = keep.tile([P, S + 2 * N], U8, name="scale_rows", align_bytes=ALIGN)
         for term, scales in enumerate((w1_scales, w3_scales)):
             cols = slice(S + N * term, S + N * (term + 1))
-            nc.sync.dma_start(scale_rows[STAGED, cols].bitcast(I32), scales[0].bitcast(I32))
+            nc.scalar.dma_start(scale_rows[STAGED, cols].bitcast(I32), scales[0].bitcast(I32))
         nc.sync.dma_start(xs_table[STAGED, :].bitcast(I32), x_scales[0].bitcast(I32))
         xw_table = keep.tile([P, T], U32, name="xw_table", align_bytes=ALIGN)
         nc.sync.dma_start(xw_table[:].bitcast(I32), words_of(x_words))
@@ -69,7 +69,8 @@ def tile_picked_lora_relu_p_kernel(
         nc.vector.tensor_copy(xs_picked[:], xs_table[:].indirect(offsets[:]))
         nc.vector.tensor_copy(scale_rows[:, 0:S].bitcast(I32), xs_picked[:].bitcast(I32))
         for r in range(PACK):
-            nc.scalar.dma_start(scale_plane[r:P:32, :].bitcast(I32), scale_rows[32 + 4 * r : 96 : 16, :].bitcast(I32))
+            queue = nc.scalar if r % 2 == 0 else nc.sync
+            queue.dma_start(scale_plane[r:P:32, :].bitcast(I32), scale_rows[32 + 4 * r : 96 : 16, :].bitcast(I32))
 
         w2_bf16 = keep.tile([P, PACK, P, PACK], BF16, name="w2_bf16", align_bytes=ALIGN)
         nc.scalar.copy(w2_bf16[:].rearrange("p t m j -> p m j t"), w2_raw[:].rearrange("p j (m t) -> p m j t", t=PACK))

@@ -1,4 +1,5 @@
 from contextlib import ExitStack
+from math import gcd, prod
 
 import concourse.mybir as mybir
 
@@ -12,11 +13,13 @@ U32 = mybir.dt.uint32
 U16 = mybir.dt.uint16
 U8 = mybir.dt.uint8
 FP8X4 = mybir.dt.float8_e4m3fn_x4
+BYTES_OF = {F32: 4, U32: 4, BF16: 2, U16: 2, U8: 1}
 RELU = mybir.ActivationFunctionType.Relu
 
 P = 128
 PACK = 4
-ALIGN = 64
+LINE_CYCLE = 256
+STATIONARY, SCALES, MOVING = 0, 64, 128
 BANKS = 8
 BANK = 512
 HALF = S // 2
@@ -42,40 +45,46 @@ def tile_picked_lora_relu_p_kernel(
     with ExitStack() as ctx:
         keep = ctx.enter_context(tc.tile_pool(name="keep", bufs=1))
         psum = ctx.enter_context(tc.psum_pool(name="psum", bufs=1))
+        ends = [0]
 
-        xs_table = keep.tile([P, T], U8, name="xs_table", align_bytes=ALIGN)
+        def new_tile(name, shape, dtype, start=0):
+            offset = -(-(ends[-1] - start) // LINE_CYCLE) * LINE_CYCLE + start
+            ends.append(offset + BYTES_OF[dtype] * prod(shape[1:]))
+            return keep.tile(shape, dtype, name=name, offset=offset, align_bytes=gcd(start, LINE_CYCLE))
+
+        xs_table = new_tile("xs_table", [P, T], U8)
         nc.vector.memset(xs_table[:].bitcast(I32), 0)
-        scale_plane = keep.tile([P, S + 2 * N], U8, name="scale_plane", align_bytes=ALIGN)
+        scale_plane = new_tile("scale_plane", [P, S + 2 * N], U8, SCALES)
         nc.vector.memset(scale_plane[:].bitcast(I32), 0)
 
-        w2_raw = keep.tile([P, PACK, H], F32, name="w2_raw")
+        w2_raw = new_tile("w2_raw", [P, PACK, H], F32)
         nc.sync.dma_start(w2_raw[:], w2.rearrange("(p j) c -> p j c", j=PACK))
-        offsets = keep.tile([P, S // 16], U16, name="offsets")
+        offsets = new_tile("offsets", [P, S // 16], U16)
         nc.sync.dma_start(offsets[:], offs)
-        scale_rows = keep.tile([P, S + 2 * N], U8, name="scale_rows", align_bytes=ALIGN)
+        scale_rows = new_tile("scale_rows", [P, S + 2 * N], U8)
         for term, scales in enumerate((w1_scales, w3_scales)):
             cols = slice(S + N * term, S + N * (term + 1))
             nc.scalar.dma_start(scale_rows[STAGED, cols].bitcast(I32), scales[0].bitcast(I32))
         nc.sync.dma_start(xs_table[STAGED, :].bitcast(I32), x_scales[0].bitcast(I32))
-        xw_table = keep.tile([P, T], U32, name="xw_table", align_bytes=ALIGN)
+        xw_table = new_tile("xw_table", [P, T], U32)
         nc.sync.dma_start(xw_table[:].bitcast(I32), words_of(x_words))
         w_words = []
         for term, packed in enumerate((w1_words, w3_words)):
-            words = keep.tile([P, N], U32, name="w_words%d" % term, align_bytes=ALIGN)
+            words = new_tile("w_words%d" % term, [P, N], U32, STATIONARY)
             nc.sync.dma_start(words[:].bitcast(I32), words_of(packed))
             w_words.append(words)
 
-        xs_picked = keep.tile([P, S], U8, name="xs_picked", align_bytes=ALIGN)
+        xs_picked = new_tile("xs_picked", [P, S], U8)
         nc.vector.tensor_copy(xs_picked[:], xs_table[:].indirect(offsets[:]))
         nc.vector.tensor_copy(scale_rows[:, 0:S].bitcast(I32), xs_picked[:].bitcast(I32))
         for r in range(PACK):
             queue = nc.scalar if r % 2 == 0 else nc.sync
             queue.dma_start(scale_plane[r:P:32, :].bitcast(I32), scale_rows[32 + 4 * r : 96 : 16, :].bitcast(I32))
 
-        w2_bf16 = keep.tile([P, PACK, P, PACK], BF16, name="w2_bf16", align_bytes=ALIGN)
+        w2_bf16 = new_tile("w2_bf16", [P, PACK, P, PACK], BF16)
         nc.scalar.copy(w2_bf16[:].rearrange("p t m j -> p m j t"), w2_raw[:].rearrange("p j (m t) -> p m j t", t=PACK))
-        w2_words = keep.tile([P, H], U32, name="w2_words", align_bytes=ALIGN)
-        w2_plane = keep.tile([P, H], U8, name="w2_plane", align_bytes=ALIGN)
+        w2_words = new_tile("w2_words", [P, H], U32, STATIONARY)
+        w2_plane = new_tile("w2_plane", [P, H], U8, SCALES)
         nc.vector.quantize_mx(
             out=w2_words[:].bitcast(FP8X4),
             scales=w2_plane[:],
@@ -84,7 +93,7 @@ def tile_picked_lora_relu_p_kernel(
 
         xw_picked = []
         for half in range(2):
-            picked = keep.tile([P, HALF], U32, name="xw_picked%d" % half, align_bytes=ALIGN)
+            picked = new_tile("xw_picked%d" % half, [P, HALF], U32, MOVING)
             entries = offsets[:, HALF // 16 * half : HALF // 16 * (half + 1)]
             nc.vector.tensor_copy(picked[:], xw_table[:].indirect(entries))
             xw_picked.append(picked)
@@ -112,9 +121,9 @@ def tile_picked_lora_relu_p_kernel(
             words = xw_picked[first // HALF][:, start : start + width].bitcast(FP8X4)
             return words, scale_plane[:, first : first + width]
 
-        h_bf16 = [keep.tile([P, PAIR, PACK], BF16, name="h_bf16_%d" % g, align_bytes=ALIGN) for g in range(PAIRS)]
-        h_words = [keep.tile([P, PAIR], U32, name="h_words%d" % g, align_bytes=ALIGN) for g in range(PAIRS)]
-        h_plane = [keep.tile([P, PAIR], U8, name="h_plane%d" % g, align_bytes=ALIGN) for g in range(PAIRS)]
+        h_bf16 = [new_tile("h_bf16_%d" % g, [P, PAIR, PACK], BF16) for g in range(PAIRS)]
+        h_words = [new_tile("h_words%d" % g, [P, PAIR], U32, MOVING) for g in range(PAIRS)]
+        h_plane = [new_tile("h_plane%d" % g, [P, PAIR], U8, SCALES) for g in range(PAIRS)]
         out_tiles = out.rearrange("(a p) s -> p a s", p=P)
 
         def first_product(c):
@@ -174,7 +183,7 @@ def tile_picked_lora_relu_p_kernel(
                     add_term(sums[:, cols], 1, a, h_words[g][:, cols].bitcast(FP8X4), h_plane[g][:, cols], cols.stop == PAIR)
 
         def store(g, a, sums, copy, queue):
-            result = keep.tile([P, PAIR], F32, name="result%d_%d" % (g, a))
+            result = new_tile("result%d_%d" % (g, a), [P, PAIR], F32)
             copy(result[:], sums)
             queue.dma_start(out_tiles[:, a, PAIR * g : PAIR * (g + 1)], result[:])
 

@@ -85,11 +85,13 @@ def tile_picked_lora_relu_p_kernel(
         nc.scalar.copy(w2_bf16[:].rearrange("p t m j -> p m j t"), w2_raw[:].rearrange("p j (m t) -> p m j t", t=PACK))
         w2_words = new_tile("w2_words", [P, H], U32, STATIONARY)
         w2_plane = new_tile("w2_plane", [P, H], U8, SCALES)
-        nc.vector.quantize_mx(
-            out=w2_words[:].bitcast(FP8X4),
-            scales=w2_plane[:],
-            in_=w2_bf16[:].rearrange("p t m j -> p (t m j)"),
-        )
+        for half in range(2):
+            cols = slice(H // 2 * half, H // 2 * (half + 1))
+            nc.vector.quantize_mx(
+                out=w2_words[:, cols].bitcast(FP8X4),
+                scales=w2_plane[:, cols],
+                in_=w2_bf16[:, 2 * half : 2 * half + 2].rearrange("p t m j -> p (t m j)"),
+            )
 
         xw_picked = []
         for half in range(2):
@@ -99,13 +101,13 @@ def tile_picked_lora_relu_p_kernel(
             xw_picked.append(picked)
 
         warm_bank = psum.tile([P, BANK], F32, name="bank%d" % (BANKS - 1))
-        for warm_pass in range(WARM_PASSES):
+        for width in [H // 2] + [H] * WARM_PASSES:
             nc.tensor.matmul_mx(
-                out=warm_bank[:],
+                out=warm_bank[:, 0:width],
                 lhsT=w2_words[:, 0:P].bitcast(FP8X4),
                 lhsT_scale=w2_plane[:, 0:P],
-                rhs=w2_words[:].bitcast(FP8X4),
-                rhs_scale=w2_plane[:],
+                rhs=w2_words[:, 0:width].bitcast(FP8X4),
+                rhs_scale=w2_plane[:, 0:width],
                 start=True,
                 stop=True,
             )

@@ -31,6 +31,7 @@ ROW_TILES = N // P
 STAGED = slice(32, 96, 4)
 AHEAD = 4
 LAG = 3
+WARM_ROWS = 32
 WARM_PASSES = 3
 
 
@@ -101,11 +102,11 @@ def tile_picked_lora_relu_p_kernel(
             xw_picked.append(picked)
 
         warm_bank = psum.tile([P, BANK], F32, name="bank%d" % (BANKS - 1))
-        for width in [H // 2] + [H] * WARM_PASSES:
+        for rows, width in [(P, H // 2)] + [(WARM_ROWS, H)] * WARM_PASSES:
             nc.tensor.matmul_mx(
-                out=warm_bank[:, 0:width],
-                lhsT=w2_words[:, 0:P].bitcast(FP8X4),
-                lhsT_scale=w2_plane[:, 0:P],
+                out=warm_bank[0:rows, 0:width],
+                lhsT=w2_words[:, 0:rows].bitcast(FP8X4),
+                lhsT_scale=w2_plane[:, 0:rows],
                 rhs=w2_words[:, 0:width].bitcast(FP8X4),
                 rhs_scale=w2_plane[:, 0:width],
                 start=True,

@@ -22,7 +22,7 @@ LINE_CYCLE = 256
 STATIONARY, SCALES, MOVING = 0, 64, 128
 BANKS = 8
 BANK = 512
-HALF = S // 2
+FIRST = 384
 CHUNK = 128
 CHUNKS = S // CHUNK
 PAIR = 2 * CHUNK
@@ -48,24 +48,35 @@ def tile_picked_lora_relu_p_kernel(
         psum = ctx.enter_context(tc.psum_pool(name="psum", bufs=1))
         ends = [0]
 
-        def new_tile(name, shape, dtype, start=0):
+        def new_bytes(count, start=0):
             offset = -(-(ends[-1] - start) // LINE_CYCLE) * LINE_CYCLE + start
-            ends.append(offset + BYTES_OF[dtype] * prod(shape[1:]))
+            ends.append(offset + count)
+            return offset
+
+        def new_tile(name, shape, dtype, start=0):
+            offset = new_bytes(BYTES_OF[dtype] * prod(shape[1:]), start)
             return keep.tile(shape, dtype, name=name, offset=offset, align_bytes=gcd(start, LINE_CYCLE))
 
-        xs_table = new_tile("xs_table", [P, T], U8)
-        nc.vector.memset(xs_table[:].bitcast(I32), 0)
-        scale_plane = new_tile("scale_plane", [P, S + 2 * N], U8, SCALES)
-        nc.vector.memset(scale_plane[:].bitcast(I32), 0)
+        def zeroed_plane(name, columns, offset, engine=nc.vector):
+            plane = keep.tile([P, columns], U8, name=name, offset=offset, align_bytes=SCALES)
+            engine.memset(plane[:].bitcast(I32), 0)
+            return plane
+
+        def load_scales(queue, plane, scales):
+            for q in range(P // 32):
+                rows = scales[0][PACK * q : PACK * (q + 1), :]
+                queue.dma_start(plane[32 * q : 32 * q + PACK, :].bitcast(I32), rows.bitcast(I32))
+
+        table_bytes = new_bytes(T + SCALES)
+        w1_plane = zeroed_plane("w1_plane", N, new_bytes(N, SCALES))
+        xs_table = zeroed_plane("xs_table", T, table_bytes)
+        x_plane = zeroed_plane("x_plane", S, new_bytes(S, SCALES))
 
         w2_raw = new_tile("w2_raw", [P, PACK, H], F32)
         nc.sync.dma_start(w2_raw[:], w2.rearrange("(p j) c -> p j c", j=PACK))
         offsets = new_tile("offsets", [P, S // 16], U16)
         nc.sync.dma_start(offsets[:], offs)
-        scale_rows = new_tile("scale_rows", [P, S + 2 * N], U8)
-        for term, scales in enumerate((w1_scales, w3_scales)):
-            cols = slice(S + N * term, S + N * (term + 1))
-            nc.scalar.dma_start(scale_rows[STAGED, cols].bitcast(I32), scales[0].bitcast(I32))
+        load_scales(nc.scalar, w1_plane, w1_scales)
         nc.sync.dma_start(xs_table[STAGED, :].bitcast(I32), x_scales[0].bitcast(I32))
         xw_table = new_tile("xw_table", [P, T], U32)
         nc.sync.dma_start(xw_table[:].bitcast(I32), words_of(x_words))
@@ -77,10 +88,13 @@ def tile_picked_lora_relu_p_kernel(
 
         xs_picked = new_tile("xs_picked", [P, S], U8)
         nc.vector.tensor_copy(xs_picked[:], xs_table[:].indirect(offsets[:]))
-        nc.vector.tensor_copy(scale_rows[:, 0:S].bitcast(I32), xs_picked[:].bitcast(I32))
         for r in range(PACK):
             queue = nc.scalar if r % 2 == 0 else nc.sync
-            queue.dma_start(scale_plane[r:P:32, :].bitcast(I32), scale_rows[32 + 4 * r : 96 : 16, :].bitcast(I32))
+            queue.dma_start(x_plane[r:P:32, :].bitcast(I32), xs_picked[32 + 4 * r : 96 : 16, :].bitcast(I32))
+
+        w3_plane = zeroed_plane("w3_plane", N, table_bytes + SCALES, nc.gpsimd)
+        load_scales(nc.sync, w3_plane, w3_scales)
+        w_planes = [w1_plane, w3_plane]
 
         w2_bf16 = new_tile("w2_bf16", [P, PACK, P, PACK], BF16)
         nc.scalar.copy(w2_bf16[:].rearrange("p t m j -> p m j t"), w2_raw[:].rearrange("p j (m t) -> p m j t", t=PACK))
@@ -94,12 +108,9 @@ def tile_picked_lora_relu_p_kernel(
                 in_=w2_bf16[:, 2 * half : 2 * half + 2].rearrange("p t m j -> p (t m j)"),
             )
 
-        xw_picked = []
-        for half in range(2):
-            picked = new_tile("xw_picked%d" % half, [P, HALF], U32, MOVING)
-            entries = offsets[:, HALF // 16 * half : HALF // 16 * (half + 1)]
-            nc.vector.tensor_copy(picked[:], xw_table[:].indirect(entries))
-            xw_picked.append(picked)
+        xw_picked = new_tile("xw_picked", [P, S], U32, MOVING)
+        for first, end in ((0, FIRST), (FIRST, S)):
+            nc.vector.tensor_copy(xw_picked[:, first:end], xw_table[:].indirect(offsets[:, first // 16 : end // 16]))
 
         warm_bank = psum.tile([P, BANK], F32, name="bank%d" % (BANKS - 1))
         for rows, width in [(P, H // 2)] + [(WARM_ROWS, H)] * WARM_PASSES:
@@ -113,16 +124,12 @@ def tile_picked_lora_relu_p_kernel(
                 stop=True,
             )
 
-        taken = []
-
-        def take_bank():
-            taken.append(psum.tile([P, BANK], F32, name="bank%d" % (len(taken) % BANKS)))
-            return taken[-1]
+        def take_bank(number):
+            return psum.tile([P, BANK], F32, name="bank%d" % number)
 
         def tokens(first, width):
-            start = first % HALF
-            words = xw_picked[first // HALF][:, start : start + width].bitcast(FP8X4)
-            return words, scale_plane[:, first : first + width]
+            cols = slice(first, first + width)
+            return xw_picked[:, cols].bitcast(FP8X4), x_plane[:, cols]
 
         h_bf16 = [new_tile("h_bf16_%d" % g, [P, PAIR, PACK], BF16) for g in range(PAIRS)]
         h_words = [new_tile("h_words%d" % g, [P, PAIR], U32, MOVING) for g in range(PAIRS)]
@@ -130,7 +137,7 @@ def tile_picked_lora_relu_p_kernel(
         out_tiles = out.rearrange("(a p) s -> p a s", p=P)
 
         def first_product(c):
-            sums = take_bank()[:].rearrange("p (t n) -> p t n", t=PACK)
+            sums = take_bank(c % (BANKS - ROW_TILES))[:].rearrange("p (t n) -> p t n", t=PACK)
             words, scales = tokens(CHUNK * c, CHUNK)
             for t in range(PACK):
                 nc.tensor.matmul_mx(
@@ -162,11 +169,10 @@ def tile_picked_lora_relu_p_kernel(
             )
 
         def add_term(sums, term, a, words, scales, stop=False):
-            first = S + N * term + P * a
             nc.tensor.matmul_mx(
                 out=sums,
                 lhsT=w_words[term][:, P * a : P * (a + 1)].bitcast(FP8X4),
-                lhsT_scale=scale_plane[:, first : first + P],
+                lhsT_scale=w_planes[term][:, P * a : P * (a + 1)],
                 rhs=words,
                 rhs_scale=scales,
                 start=(term == 0),
@@ -174,7 +180,7 @@ def tile_picked_lora_relu_p_kernel(
             )
 
         def open_groups(g):
-            groups = [take_bank()[:, 0:PAIR] for a in range(ROW_TILES)]
+            groups = [take_bank(ROW_TILES * ((g + 2) % 3 + 1) + a)[:, 0:PAIR] for a in range(ROW_TILES)]
             for a, sums in enumerate(groups):
                 add_term(sums, 0, a, *tokens(PAIR * g, PAIR))
             return groups
@@ -193,8 +199,9 @@ def tile_picked_lora_relu_p_kernel(
         def on_vector(i):
             return i % 3 == 1
 
-        h_sums = [first_product(c) for c in range(AHEAD)]
-        groups = []
+        h_sums = [first_product(c) for c in range(FIRST // CHUNK)]
+        groups = [open_groups(0)]
+        h_sums.extend(first_product(c) for c in range(FIRST // CHUNK, AHEAD))
         for c in range(CHUNKS + 1 + LAG):
             if c < CHUNKS:
                 relu_round(c, h_sums[c], on_scalar=not on_vector(c))
@@ -204,7 +211,7 @@ def tile_picked_lora_relu_p_kernel(
                 close_groups(c // 2 - 1, groups[-1])
             if c + AHEAD < CHUNKS:
                 h_sums.append(first_product(c + AHEAD))
-            if c < CHUNKS and c % 2 == 1:
+            if 1 < c < CHUNKS and c % 2 == 1:
                 groups.append(open_groups(c // 2))
             if c - LAG >= 2 and (c - LAG) % 2 == 0:
                 g = (c - LAG) // 2 - 1

@@ -57,44 +57,38 @@ def tile_picked_lora_relu_p_kernel(
             offset = new_bytes(BYTES_OF[dtype] * prod(shape[1:]), start)
             return keep.tile(shape, dtype, name=name, offset=offset, align_bytes=gcd(start, LINE_CYCLE))
 
-        def zeroed_plane(name, columns, offset, engine=nc.vector):
+        def zeroed_plane(name, columns, offset):
             plane = keep.tile([P, columns], U8, name=name, offset=offset, align_bytes=SCALES)
-            engine.memset(plane[:].bitcast(I32), 0)
+            nc.vector.memset(plane[:].bitcast(I32), 0)
             return plane
 
-        def load_scales(queue, plane, scales):
-            for q in range(P // 32):
-                rows = scales[0][PACK * q : PACK * (q + 1), :]
-                queue.dma_start(plane[32 * q : 32 * q + PACK, :].bitcast(I32), rows.bitcast(I32))
-
-        table_bytes = new_bytes(T + SCALES)
-        w1_plane = zeroed_plane("w1_plane", N, new_bytes(N, SCALES))
-        xs_table = zeroed_plane("xs_table", T, table_bytes)
+        xs_table = zeroed_plane("xs_table", T, new_bytes(T))
         x_plane = zeroed_plane("x_plane", S, new_bytes(S, SCALES))
+        w_plane = zeroed_plane("w_plane", 2 * N, new_bytes(2 * N, SCALES))
 
         w2_raw = new_tile("w2_raw", [P, PACK, H], F32)
         nc.sync.dma_start(w2_raw[:], w2.rearrange("(p j) c -> p j c", j=PACK))
         offsets = new_tile("offsets", [P, S // 16], U16)
         nc.sync.dma_start(offsets[:], offs)
-        load_scales(nc.scalar, w1_plane, w1_scales)
         nc.sync.dma_start(xs_table[STAGED, :].bitcast(I32), x_scales[0].bitcast(I32))
         xw_table = new_tile("xw_table", [P, T], U32)
         nc.sync.dma_start(xw_table[:].bitcast(I32), words_of(x_words))
-        w_words = []
-        for term, packed in enumerate((w1_words, w3_words)):
-            words = new_tile("w_words%d" % term, [P, N], U32, STATIONARY)
-            nc.sync.dma_start(words[:].bitcast(I32), words_of(packed))
-            w_words.append(words)
+        ws_staged = new_tile("ws_staged", [P, 2 * N], U8)
+        for term, scales in enumerate((w1_scales, w3_scales)):
+            nc.sync.dma_start(ws_staged[STAGED, N * term : N * (term + 1)].bitcast(I32), scales[0].bitcast(I32))
+
+        def place_rows(plane, staged):
+            for r in range(PACK):
+                queue = nc.scalar if r % 2 == 0 else nc.sync
+                queue.dma_start(plane[r:P:32, :].bitcast(I32), staged[32 + 4 * r : 96 : 16, :].bitcast(I32))
 
         xs_picked = new_tile("xs_picked", [P, S], U8)
         nc.vector.tensor_copy(xs_picked[:], xs_table[:].indirect(offsets[:]))
-        for r in range(PACK):
-            queue = nc.scalar if r % 2 == 0 else nc.sync
-            queue.dma_start(x_plane[r:P:32, :].bitcast(I32), xs_picked[32 + 4 * r : 96 : 16, :].bitcast(I32))
-
-        w3_plane = zeroed_plane("w3_plane", N, table_bytes + SCALES, nc.gpsimd)
-        load_scales(nc.sync, w3_plane, w3_scales)
-        w_planes = [w1_plane, w3_plane]
+        place_rows(x_plane, xs_picked)
+        w_words = [new_tile("w_words%d" % term, [P, N], U32, STATIONARY) for term in range(2)]
+        nc.sync.dma_start(w_words[0][:].bitcast(I32), words_of(w1_words))
+        place_rows(w_plane, ws_staged)
+        nc.sync.dma_start(w_words[1][:].bitcast(I32), words_of(w3_words))
 
         w2_bf16 = new_tile("w2_bf16", [P, PACK, P, PACK], BF16)
         nc.scalar.copy(w2_bf16[:].rearrange("p t m j -> p m j t"), w2_raw[:].rearrange("p j (m t) -> p m j t", t=PACK))
@@ -172,7 +166,7 @@ def tile_picked_lora_relu_p_kernel(
             nc.tensor.matmul_mx(
                 out=sums,
                 lhsT=w_words[term][:, P * a : P * (a + 1)].bitcast(FP8X4),
-                lhsT_scale=w_planes[term][:, P * a : P * (a + 1)],
+                lhsT_scale=w_plane[:, N * term + P * a : N * term + P * (a + 1)],
                 rhs=words,
                 rhs_scale=scales,
                 start=(term == 0),

@@ -22,15 +22,15 @@ LINE_CYCLE = 256
 STATIONARY, SCALES, MOVING = 0, 64, 128
 BANKS = 8
 BANK = 512
-FIRST = 384
+GATHER = 256
 CHUNK = 128
 CHUNKS = S // CHUNK
 PAIR = 2 * CHUNK
 PAIRS = S // PAIR
 ROW_TILES = N // P
 STAGED = slice(32, 96, 4)
-AHEAD = 4
-LAG = 3
+H_BANKS = (0, 1, 2, 3, 4, 5, 0, 1)
+OUT_BANKS = ((6, 7), (2, 3), (4, 5), (6, 7))
 WARM_ROWS = 32
 WARM_PASSES = 3
 
@@ -57,38 +57,44 @@ def tile_picked_lora_relu_p_kernel(
             offset = new_bytes(BYTES_OF[dtype] * prod(shape[1:]), start)
             return keep.tile(shape, dtype, name=name, offset=offset, align_bytes=gcd(start, LINE_CYCLE))
 
-        def zeroed_plane(name, columns, offset):
+        def zeroed_plane(name, columns, offset, engine=nc.vector):
             plane = keep.tile([P, columns], U8, name=name, offset=offset, align_bytes=SCALES)
-            nc.vector.memset(plane[:].bitcast(I32), 0)
+            engine.memset(plane[:].bitcast(I32), 0)
             return plane
 
-        xs_table = zeroed_plane("xs_table", T, new_bytes(T))
+        def load_scales(queue, plane, scales):
+            for q in range(P // 32):
+                rows = scales[0][PACK * q : PACK * (q + 1), :]
+                queue.dma_start(plane[32 * q : 32 * q + PACK, :].bitcast(I32), rows.bitcast(I32))
+
+        table_bytes = new_bytes(T + SCALES)
+        w1_plane = zeroed_plane("w1_plane", N, new_bytes(N, SCALES))
+        xs_table = zeroed_plane("xs_table", T, table_bytes)
         x_plane = zeroed_plane("x_plane", S, new_bytes(S, SCALES))
-        w_plane = zeroed_plane("w_plane", 2 * N, new_bytes(2 * N, SCALES))
 
         w2_raw = new_tile("w2_raw", [P, PACK, H], F32)
         nc.sync.dma_start(w2_raw[:], w2.rearrange("(p j) c -> p j c", j=PACK))
         offsets = new_tile("offsets", [P, S // 16], U16)
         nc.sync.dma_start(offsets[:], offs)
+        load_scales(nc.scalar, w1_plane, w1_scales)
         nc.sync.dma_start(xs_table[STAGED, :].bitcast(I32), x_scales[0].bitcast(I32))
         xw_table = new_tile("xw_table", [P, T], U32)
         nc.sync.dma_start(xw_table[:].bitcast(I32), words_of(x_words))
-        ws_staged = new_tile("ws_staged", [P, 2 * N], U8)
-        for term, scales in enumerate((w1_scales, w3_scales)):
-            nc.sync.dma_start(ws_staged[STAGED, N * term : N * (term + 1)].bitcast(I32), scales[0].bitcast(I32))
-
-        def place_rows(plane, staged):
-            for r in range(PACK):
-                queue = nc.scalar if r % 2 == 0 else nc.sync
-                queue.dma_start(plane[r:P:32, :].bitcast(I32), staged[32 + 4 * r : 96 : 16, :].bitcast(I32))
+        w_words = []
+        for term, packed in enumerate((w1_words, w3_words)):
+            words = new_tile("w_words%d" % term, [P, N], U32, STATIONARY)
+            nc.sync.dma_start(words[:].bitcast(I32), words_of(packed))
+            w_words.append(words)
 
         xs_picked = new_tile("xs_picked", [P, S], U8)
         nc.vector.tensor_copy(xs_picked[:], xs_table[:].indirect(offsets[:]))
-        place_rows(x_plane, xs_picked)
-        w_words = [new_tile("w_words%d" % term, [P, N], U32, STATIONARY) for term in range(2)]
-        nc.sync.dma_start(w_words[0][:].bitcast(I32), words_of(w1_words))
-        place_rows(w_plane, ws_staged)
-        nc.sync.dma_start(w_words[1][:].bitcast(I32), words_of(w3_words))
+        for r in range(PACK):
+            queue = nc.scalar if r % 2 == 0 else nc.sync
+            queue.dma_start(x_plane[r:P:32, :].bitcast(I32), xs_picked[32 + 4 * r : 96 : 16, :].bitcast(I32))
+
+        w3_plane = zeroed_plane("w3_plane", N, table_bytes + SCALES, nc.gpsimd)
+        load_scales(nc.sync, w3_plane, w3_scales)
+        w_planes = [w1_plane, w3_plane]
 
         w2_bf16 = new_tile("w2_bf16", [P, PACK, P, PACK], BF16)
         nc.scalar.copy(w2_bf16[:].rearrange("p t m j -> p m j t"), w2_raw[:].rearrange("p j (m t) -> p m j t", t=PACK))
@@ -103,7 +109,8 @@ def tile_picked_lora_relu_p_kernel(
             )
 
         xw_picked = new_tile("xw_picked", [P, S], U32, MOVING)
-        for first, end in ((0, FIRST), (FIRST, S)):
+        for first in range(0, S, GATHER):
+            end = first + GATHER
             nc.vector.tensor_copy(xw_picked[:, first:end], xw_table[:].indirect(offsets[:, first // 16 : end // 16]))
 
         warm_bank = psum.tile([P, BANK], F32, name="bank%d" % (BANKS - 1))
@@ -131,7 +138,7 @@ def tile_picked_lora_relu_p_kernel(
         out_tiles = out.rearrange("(a p) s -> p a s", p=P)
 
         def first_product(c):
-            sums = take_bank(c % (BANKS - ROW_TILES))[:].rearrange("p (t n) -> p t n", t=PACK)
+            sums = take_bank(H_BANKS[c])[:].rearrange("p (t n) -> p t n", t=PACK)
             words, scales = tokens(CHUNK * c, CHUNK)
             for t in range(PACK):
                 nc.tensor.matmul_mx(
@@ -166,7 +173,7 @@ def tile_picked_lora_relu_p_kernel(
             nc.tensor.matmul_mx(
                 out=sums,
                 lhsT=w_words[term][:, P * a : P * (a + 1)].bitcast(FP8X4),
-                lhsT_scale=w_plane[:, N * term + P * a : N * term + P * (a + 1)],
+                lhsT_scale=w_planes[term][:, P * a : P * (a + 1)],
                 rhs=words,
                 rhs_scale=scales,
                 start=(term == 0),
@@ -174,7 +181,7 @@ def tile_picked_lora_relu_p_kernel(
             )
 
         def open_groups(g):
-            groups = [take_bank(ROW_TILES * ((g + 2) % 3 + 1) + a)[:, 0:PAIR] for a in range(ROW_TILES)]
+            groups = [take_bank(OUT_BANKS[g][a])[:, 0:PAIR] for a in range(ROW_TILES)]
             for a, sums in enumerate(groups):
                 add_term(sums, 0, a, *tokens(PAIR * g, PAIR))
             return groups
@@ -190,29 +197,48 @@ def tile_picked_lora_relu_p_kernel(
             copy(result[:], sums)
             queue.dma_start(out_tiles[:, a, PAIR * g : PAIR * (g + 1)], result[:])
 
-        def on_vector(i):
-            return i % 3 == 1
+        def leave(g, a, on_scalar, queue=nc.sync):
+            store(g, a, groups[g][a], nc.scalar.copy if on_scalar else nc.vector.tensor_copy, queue)
 
-        h_sums = [first_product(c) for c in range(FIRST // CHUNK)]
-        groups = [open_groups(0)]
-        h_sums.extend(first_product(c) for c in range(FIRST // CHUNK, AHEAD))
-        for c in range(CHUNKS + 1 + LAG):
-            if c < CHUNKS:
-                relu_round(c, h_sums[c], on_scalar=not on_vector(c))
-            if 1 <= c <= CHUNKS:
-                quantise_h(c - 1)
-            if 2 <= c <= CHUNKS and c % 2 == 0:
-                close_groups(c // 2 - 1, groups[-1])
-            if c + AHEAD < CHUNKS:
-                h_sums.append(first_product(c + AHEAD))
-            if 1 < c < CHUNKS and c % 2 == 1:
-                groups.append(open_groups(c // 2))
-            if c - LAG >= 2 and (c - LAG) % 2 == 0:
-                g = (c - LAG) // 2 - 1
-                if g < PAIRS - 1:
-                    for a in range(ROW_TILES):
-                        copy = nc.vector.tensor_copy if on_vector(ROW_TILES * g + a) else nc.scalar.copy
-                        store(g, a, groups[g][a], copy, nc.sync)
-                else:
-                    store(g, 0, groups[g][0], nc.vector.tensor_copy, nc.sync)
-                    store(g, 1, groups[g][1], nc.scalar.copy, nc.scalar)
+        h_sums = [None] * CHUNKS
+        groups = [None] * PAIRS
+        h_sums[0] = first_product(0)
+        h_sums[1] = first_product(1)
+        h_sums[2] = first_product(2)
+        h_sums[3] = first_product(3)
+        groups[0] = open_groups(0)
+        h_sums[4] = first_product(4)
+        h_sums[5] = first_product(5)
+        relu_round(0, h_sums[0], True)
+        relu_round(1, h_sums[1], True)
+        quantise_h(0)
+        quantise_h(1)
+        close_groups(0, groups[0])
+        h_sums[6] = first_product(6)
+        relu_round(2, h_sums[2], True)
+        relu_round(4, h_sums[4], False)
+        h_sums[7] = first_product(7)
+        relu_round(3, h_sums[3], True)
+        quantise_h(2)
+        quantise_h(3)
+        groups[1] = open_groups(1)
+        close_groups(1, groups[1])
+        leave(0, 0, False)
+        relu_round(5, h_sums[5], True)
+        quantise_h(4)
+        quantise_h(5)
+        leave(0, 1, True)
+        groups[2] = open_groups(2)
+        close_groups(2, groups[2])
+        groups[3] = open_groups(3)
+        relu_round(6, h_sums[6], True)
+        relu_round(7, h_sums[7], False)
+        quantise_h(6)
+        quantise_h(7)
+        close_groups(3, groups[3])
+        leave(1, 0, True)
+        leave(1, 1, True)
+        leave(2, 0, True)
+        leave(2, 1, True)
+        leave(3, 0, False)
+        leave(3, 1, True, nc.scalar)

@@ -100,12 +100,12 @@ def tile_picked_lora_relu_p_kernel(
         nc.scalar.copy(w2_bf16[:].rearrange("p t m j -> p m j t"), w2_raw[:].rearrange("p j (m t) -> p m j t", t=PACK))
         w2_words = new_tile("w2_words", [P, H], U32, STATIONARY)
         w2_plane = new_tile("w2_plane", [P, H], U8, SCALES)
-        for half in range(2):
-            cols = slice(H // 2 * half, H // 2 * (half + 1))
+        for first, end in ((0, 1), (1, 2), (2, PACK)):
+            cols = slice(P * first, P * end)
             nc.vector.quantize_mx(
                 out=w2_words[:, cols].bitcast(FP8X4),
                 scales=w2_plane[:, cols],
-                in_=w2_bf16[:, 2 * half : 2 * half + 2].rearrange("p t m j -> p (t m j)"),
+                in_=w2_bf16[:, first:end].rearrange("p t m j -> p (t m j)"),
             )
 
         xw_picked = new_tile("xw_picked", [P, S], U32, MOVING)
@@ -114,7 +114,7 @@ def tile_picked_lora_relu_p_kernel(
             nc.vector.tensor_copy(xw_picked[:, first:end], xw_table[:].indirect(offsets[:, first // 16 : end // 16]))
 
         warm_bank = psum.tile([P, BANK], F32, name="bank%d" % (BANKS - 1))
-        for rows, width in [(P, H // 2)] + [(WARM_ROWS, H)] * WARM_PASSES:
+        for rows, width in [(WARM_ROWS, P)] * 2 + [(P, H // 2)] + [(WARM_ROWS, H)] * WARM_PASSES:
             nc.tensor.matmul_mx(
                 out=warm_bank[0:rows, 0:width],
                 lhsT=w2_words[:, 0:rows].bitcast(FP8X4),

@@ -68,8 +68,8 @@ def tile_picked_lora_relu_p_kernel(
                 queue.dma_start(plane[32 * q : 32 * q + PACK, :].bitcast(I32), rows.bitcast(I32))
 
         table_bytes = new_bytes(T + SCALES)
-        w1_plane = zeroed_plane("w1_plane", N, new_bytes(N, SCALES))
         xs_table = zeroed_plane("xs_table", T, table_bytes)
+        w1_plane = zeroed_plane("w1_plane", N, new_bytes(N, SCALES), nc.gpsimd)
         x_plane = zeroed_plane("x_plane", S, new_bytes(S, SCALES))
 
         w2_raw = new_tile("w2_raw", [P, PACK, H], F32)

@@ -89,11 +89,10 @@ def tile_picked_lora_relu_p_kernel(
         xs_picked = new_tile("xs_picked", [P, S], U8)
         nc.vector.tensor_copy(xs_picked[:], xs_table[:].indirect(offsets[:]))
         for r in range(PACK):
-            queue = nc.scalar if r % 2 == 0 else nc.sync
-            queue.dma_start(x_plane[r:P:32, :].bitcast(I32), xs_picked[32 + 4 * r : 96 : 16, :].bitcast(I32))
+            nc.scalar.dma_start(x_plane[r:P:32, :].bitcast(I32), xs_picked[32 + 4 * r : 96 : 16, :].bitcast(I32))
 
         w3_plane = zeroed_plane("w3_plane", N, table_bytes + SCALES, nc.gpsimd)
-        load_scales(nc.sync, w3_plane, w3_scales)
+        load_scales(nc.scalar, w3_plane, w3_scales)
         w_planes = [w1_plane, w3_plane]
 
         w2_bf16 = new_tile("w2_bf16", [P, PACK, P, PACK], BF16)

from contextlib import ExitStack
from math import gcd, prod

import concourse.mybir as mybir

K, T, S, H, N = 512, 4096, 1024, 512, 256
FLOPS = 2 * S * (K * H + K * N + H * N)

F32 = mybir.dt.float32
BF16 = mybir.dt.bfloat16
I32 = mybir.dt.int32
U32 = mybir.dt.uint32
U16 = mybir.dt.uint16
U8 = mybir.dt.uint8
FP8X4 = mybir.dt.float8_e4m3fn_x4
BYTES_OF = {F32: 4, U32: 4, BF16: 2, U16: 2, U8: 1}
RELU = mybir.ActivationFunctionType.Relu

P = 128
PACK = 4
LINE_CYCLE = 256
STATIONARY, SCALES, MOVING = 0, 64, 128
BANKS = 8
BANK = 512
GATHER = 256
CHUNK = 128
CHUNKS = S // CHUNK
PAIR = 2 * CHUNK
PAIRS = S // PAIR
ROW_TILES = N // P
STAGED = slice(32, 96, 4)
H_BANKS = (0, 1, 2, 3, 4, 5, 0, 1)
OUT_BANKS = ((6, 7), (2, 3), (4, 5), (6, 7))
WARM_ROWS = 32
WARM_PASSES = 3


def words_of(packed):
    return packed[0].rearrange("p n t -> p (n t)").bitcast(I32)


def tile_picked_lora_relu_p_kernel(
    tc, x_words, x_scales, w1_words, w1_scales, w2, w3_words, w3_scales, offs, out
):
    nc = tc.nc
    with ExitStack() as ctx:
        keep = ctx.enter_context(tc.tile_pool(name="keep", bufs=1))
        psum = ctx.enter_context(tc.psum_pool(name="psum", bufs=1))
        ends = [0]

        def new_bytes(count, start=0):
            offset = -(-(ends[-1] - start) // LINE_CYCLE) * LINE_CYCLE + start
            ends.append(offset + count)
            return offset

        def new_tile(name, shape, dtype, start=0):
            offset = new_bytes(BYTES_OF[dtype] * prod(shape[1:]), start)
            return keep.tile(shape, dtype, name=name, offset=offset, align_bytes=gcd(start, LINE_CYCLE))

        def zeroed_plane(name, columns, offset, engine=nc.vector):
            plane = keep.tile([P, columns], U8, name=name, offset=offset, align_bytes=SCALES)
            engine.memset(plane[:].bitcast(I32), 0)
            return plane

        def load_scales(queue, plane, scales):
            for q in range(P // 32):
                rows = scales[0][PACK * q : PACK * (q + 1), :]
                queue.dma_start(plane[32 * q : 32 * q + PACK, :].bitcast(I32), rows.bitcast(I32))

        table_bytes = new_bytes(T + SCALES)
        xs_table = zeroed_plane("xs_table", T, table_bytes)
        w1_plane = zeroed_plane("w1_plane", N, new_bytes(N, SCALES), nc.gpsimd)
        x_plane = zeroed_plane("x_plane", S, new_bytes(S, SCALES))

        w2_raw = new_tile("w2_raw", [P, PACK, H], F32)
        nc.sync.dma_start(w2_raw[:], w2.rearrange("(p j) c -> p j c", j=PACK))
        offsets = new_tile("offsets", [P, S // 16], U16)
        nc.sync.dma_start(offsets[:], offs)
        load_scales(nc.scalar, w1_plane, w1_scales)
        nc.sync.dma_start(xs_table[STAGED, :].bitcast(I32), x_scales[0].bitcast(I32))
        xw_table = new_tile("xw_table", [P, T], U32)
        nc.sync.dma_start(xw_table[:].bitcast(I32), words_of(x_words))
        w_words = []
        for term, packed in enumerate((w1_words, w3_words)):
            words = new_tile("w_words%d" % term, [P, N], U32, STATIONARY)
            nc.sync.dma_start(words[:].bitcast(I32), words_of(packed))
            w_words.append(words)

        xs_picked = new_tile("xs_picked", [P, S], U8)
        nc.vector.tensor_copy(xs_picked[:], xs_table[:].indirect(offsets[:]))
        for r in range(PACK):
            nc.scalar.dma_start(x_plane[r:P:32, :].bitcast(I32), xs_picked[32 + 4 * r : 96 : 16, :].bitcast(I32))

        w3_plane = zeroed_plane("w3_plane", N, table_bytes + SCALES, nc.gpsimd)
        load_scales(nc.scalar, w3_plane, w3_scales)
        w_planes = [w1_plane, w3_plane]

        w2_bf16 = new_tile("w2_bf16", [P, PACK, P, PACK], BF16)
        nc.scalar.copy(w2_bf16[:].rearrange("p t m j -> p m j t"), w2_raw[:].rearrange("p j (m t) -> p m j t", t=PACK))
        w2_words = new_tile("w2_words", [P, H], U32, STATIONARY)
        w2_plane = new_tile("w2_plane", [P, H], U8, SCALES)
        for first, end in ((0, 1), (1, 2), (2, PACK)):
            cols = slice(P * first, P * end)
            nc.vector.quantize_mx(
                out=w2_words[:, cols].bitcast(FP8X4),
                scales=w2_plane[:, cols],
                in_=w2_bf16[:, first:end].rearrange("p t m j -> p (t m j)"),
            )

        xw_picked = new_tile("xw_picked", [P, S], U32, MOVING)
        for first in range(0, S, GATHER):
            end = first + GATHER
            nc.vector.tensor_copy(xw_picked[:, first:end], xw_table[:].indirect(offsets[:, first // 16 : end // 16]))

        warm_bank = psum.tile([P, BANK], F32, name="bank%d" % (BANKS - 1))
        for rows, width in [(WARM_ROWS, P)] * 2 + [(P, H // 2)] + [(WARM_ROWS, H)] * WARM_PASSES:
            nc.tensor.matmul_mx(
                out=warm_bank[0:rows, 0:width],
                lhsT=w2_words[:, 0:rows].bitcast(FP8X4),
                lhsT_scale=w2_plane[:, 0:rows],
                rhs=w2_words[:, 0:width].bitcast(FP8X4),
                rhs_scale=w2_plane[:, 0:width],
                start=True,
                stop=True,
            )

        def take_bank(number):
            return psum.tile([P, BANK], F32, name="bank%d" % number)

        def tokens(first, width):
            cols = slice(first, first + width)
            return xw_picked[:, cols].bitcast(FP8X4), x_plane[:, cols]

        h_bf16 = [new_tile("h_bf16_%d" % g, [P, PAIR, PACK], BF16) for g in range(PAIRS)]
        h_words = [new_tile("h_words%d" % g, [P, PAIR], U32, MOVING) for g in range(PAIRS)]
        h_plane = [new_tile("h_plane%d" % g, [P, PAIR], U8, SCALES) for g in range(PAIRS)]
        out_tiles = out.rearrange("(a p) s -> p a s", p=P)

        def first_product(c):
            sums = take_bank(H_BANKS[c])[:].rearrange("p (t n) -> p t n", t=PACK)
            words, scales = tokens(CHUNK * c, CHUNK)
            for t in range(PACK):
                nc.tensor.matmul_mx(
                    out=sums[:, t, :],
                    lhsT=w2_words[:, P * t : P * (t + 1)].bitcast(FP8X4),
                    lhsT_scale=w2_plane[:, P * t : P * (t + 1)],
                    rhs=words,
                    rhs_scale=scales,
                    start=True,
                    stop=True,
                )
            return sums

        def in_pair(c):
            return slice(CHUNK * (c % 2), CHUNK * (c % 2 + 1))

        def relu_round(c, sums, on_scalar):
            rounded = h_bf16[c // 2][:, in_pair(c), :]
            if on_scalar:
                nc.scalar.activation(rounded, sums.rearrange("p t n -> p n t"), RELU)
            else:
                nc.vector.tensor_scalar_max(rounded, sums.rearrange("p t n -> p n t"), 0.0)

        def quantise_h(c):
            nc.vector.quantize_mx(
                out=h_words[c // 2][:, in_pair(c)].bitcast(FP8X4),
                scales=h_plane[c // 2][:, in_pair(c)],
                in_=h_bf16[c // 2][:, in_pair(c), :].rearrange("p n t -> p (n t)"),
            )

        def add_term(sums, term, a, words, scales, stop=False):
            nc.tensor.matmul_mx(
                out=sums,
                lhsT=w_words[term][:, P * a : P * (a + 1)].bitcast(FP8X4),
                lhsT_scale=w_planes[term][:, P * a : P * (a + 1)],
                rhs=words,
                rhs_scale=scales,
                start=(term == 0),
                stop=stop,
            )

        def open_groups(g):
            groups = [take_bank(OUT_BANKS[g][a])[:, 0:PAIR] for a in range(ROW_TILES)]
            for a, sums in enumerate(groups):
                add_term(sums, 0, a, *tokens(PAIR * g, PAIR))
            return groups

        def close_groups(g, groups):
            parts = [in_pair(0), in_pair(1)] if g == PAIRS - 1 else [slice(0, PAIR)]
            for cols in parts:
                for a, sums in enumerate(groups):
                    add_term(sums[:, cols], 1, a, h_words[g][:, cols].bitcast(FP8X4), h_plane[g][:, cols], cols.stop == PAIR)

        def store(g, a, sums, copy, queue):
            result = new_tile("result%d_%d" % (g, a), [P, PAIR], F32)
            copy(result[:], sums)
            queue.dma_start(out_tiles[:, a, PAIR * g : PAIR * (g + 1)], result[:])

        def leave(g, a, on_scalar, queue=nc.sync):
            store(g, a, groups[g][a], nc.scalar.copy if on_scalar else nc.vector.tensor_copy, queue)

        h_sums = [None] * CHUNKS
        groups = [None] * PAIRS
        h_sums[0] = first_product(0)
        h_sums[1] = first_product(1)
        h_sums[2] = first_product(2)
        h_sums[3] = first_product(3)
        groups[0] = open_groups(0)
        h_sums[4] = first_product(4)
        h_sums[5] = first_product(5)
        relu_round(0, h_sums[0], True)
        relu_round(1, h_sums[1], True)
        quantise_h(0)
        quantise_h(1)
        close_groups(0, groups[0])
        h_sums[6] = first_product(6)
        relu_round(2, h_sums[2], True)
        relu_round(4, h_sums[4], False)
        h_sums[7] = first_product(7)
        relu_round(3, h_sums[3], True)
        quantise_h(2)
        quantise_h(3)
        groups[1] = open_groups(1)
        close_groups(1, groups[1])
        leave(0, 0, False)
        relu_round(5, h_sums[5], True)
        quantise_h(4)
        quantise_h(5)
        leave(0, 1, True)
        groups[2] = open_groups(2)
        close_groups(2, groups[2])
        groups[3] = open_groups(3)
        relu_round(6, h_sums[6], True)
        relu_round(7, h_sums[7], False)
        quantise_h(6)
        quantise_h(7)
        close_groups(3, groups[3])
        leave(1, 0, True)
        leave(1, 1, True)
        leave(2, 0, True)
        leave(2, 1, True)
        leave(3, 0, False)
        leave(3, 1, True, nc.scalar)
